import numpy as np, ml_dtypes
CORES = [3,11,19,27,35,43,51,59]
N = 8
BF = ml_dtypes.bfloat16
def gentries(a):
    return np.ascontiguousarray(a.reshape(8, 16, -1).transpose(0, 2, 1)).reshape(8, -1)
def gtable(e):
    e = np.asarray(e); return np.ascontiguousarray(e.reshape(8, -1, 16).transpose(0, 2, 1)).reshape(128, -1).astype(np.int32)
V, DV, M, DC, IT, CAP, B = 256, 4, 128, 8, 2, 160, 51
E = V * DV
def mixed(rng):
    c = np.full((N, N), E // N)
    for i in range(6 * N):
        p, p2 = rng.permutation(N)[:2]; q, q2 = rng.permutation(N)[:2]
        t = rng.integers(0, min(c[p, q2], c[p2, q], CAP - c[p, q], CAP - c[p2, q2]) + 1)
        c[p, q] += t; c[p2, q2] += t; c[p, q2] -= t; c[p2, q] -= t
    return c
def fullest(rng):
    odd = np.add.outer(rng.permutation(N), rng.permutation(N)) % 2
    return E // N + (CAP - E // N) * (1 - 2 * odd)
def fewest(rng):
    low = max(0, E - (N - 1) * CAP); each = (E - low) // (N - 1); more = E - low - each * (N - 1)
    w = np.concatenate([[low], each + (np.arange(N - 1) < more)]); k = rng.integers(1, N); p = np.arange(N)
    c = np.zeros((N, N), np.int64)
    for i in range(N): c[p, (p + k + i) % N] = w[i]
    return c
def graph(rng, ways, near=False, holes=False):
    sn = rng.integers(0, V, (N, 8, N * CAP)); pl = np.zeros((N, 8, E), np.int64); vl = np.zeros((N, 8, E), np.int64)
    def order(n, d):
        return np.add.outer(rng.permutation(n), n * np.arange(d)).reshape(-1) if near else rng.permutation(n * d)
    ve = [[order(V, DV) for r in range(N)] for g in range(8)]; ce = [[order(M, DC) for r in range(N)] for g in range(8)]
    c = ways(rng); va = np.add.accumulate(c, axis=1) - c; ca = np.add.accumulate(c, axis=0) - c
    for g in range(8):
        for p in range(N):
            for q in range(N):
                h = (g + p * q) % 8; n = int(c[p, q]); s = rng.permutation(CAP if holes else n)[:n]
                a = ve[g][p][va[p, q]:va[p, q] + n]; b = ce[h][q][ca[p, q]:ca[p, q] + n]
                vl[p, g, a] = q * CAP + s; pl[q, h, b] = p * CAP + s; sn[p, g, q * CAP + s] = a % V
    return {"sn": np.stack([gtable(e) for e in sn]), "pl": np.stack([gtable(e) for e in pl]), "vl": np.stack([gtable(e) for e in vl])}
def heard(rng):
    k = np.stack([rng.permutation(16) for g in range(8)]).reshape(1, 128, 1)
    mean = B * np.array([0, 0.1, 0.2, 0.7])[k // 4]; noise = B * np.array([0.1, 0.2, 0.4, 0.6])[k % 4]
    return (np.clip(np.rint(mean + noise * rng.standard_normal((N, 128, V))), -B, B) + 0.0).astype(BF)
def setup_inputs(rng):
    return {"x": heard(rng), **graph(rng, mixed)}
def setup_inputs_full(rng):
    return {"x": heard(rng), **graph(rng, fullest)}
def setup_inputs_holes(rng):
    return {"x": heard(rng), **graph(rng, fewest, holes=True)}
def setup_inputs_ties(rng):
    k = np.stack([rng.permutation(16) for g in range(8)]).reshape(1, 128, 1) % 4; z = (N, 128, V)
    sg = 2 * rng.integers(0, 2, z) - 1
    v = np.where(k == 0, sg, np.where(k == 1, rng.integers(-2, 3, z), np.where(k == 2, np.where(rng.random(z) < 0.1, -B, B), np.where(rng.random(z) < 0.0625, 0, B * sg))))
    return {"x": v.astype(BF), **graph(rng, mixed)}
def setup_inputs_twins(rng):
    return {"x": heard(rng), **graph(rng, mixed, near=True)}
def setup_inputs_spread(rng):
    hi = B >> rng.integers(0, 6, (N, 128, 1)); hi[:, ::16] = B
    v = rng.integers(-hi, hi + 1, (N, 128, V)) * (rng.random((N, 1, V)) > 0.0625)
    return {"x": v.astype(BF), **graph(rng, mixed, holes=True)}
def check_inputs(d):
    bad = []
    try:
        x = np.asarray(d["x"]).astype(np.float64)
        if not (np.isfinite(x).all() and (x == np.rint(x)).all() and (np.abs(x) <= B).all()): bad.append("x is whole and within B")
        sn, pl, vl = [np.stack([gentries(np.asarray(d[k][r])) for r in range(N)]).astype(np.int64) for k in ("sn", "pl", "vl")]
        if sn.min() < 0 or sn.max() >= V: bad.append("sn in range")
        if min(pl.min(), vl.min()) < 0 or max(pl.max(), vl.max()) >= N * CAP: return bad + ["pl and vl in range"]
        name = True; v = np.arange(E) % V
        uv = np.zeros((8, N, N * CAP), np.int64); uc = np.zeros((8, N, N * CAP), np.int64)
        for g in range(8):
            for r in range(N):
                uv[g, r] = np.bincount(vl[r, g], minlength=N * CAP); uc[g, r] = np.bincount(pl[r, g], minlength=N * CAP)
                name = name and bool((sn[r, g][vl[r, g]] == v).all())
        a = np.arange(N); h = (np.arange(8)[:, None, None] + np.multiply.outer(a, a)) % 8
        there = uc.reshape(8, N, N, CAP).transpose(0, 2, 1, 3)[h, a[:, None], a] > 0
        if max(uv.max(), uc.max()) > 1: bad.append("entries of pl and of vl differ")
        if not ((uv.reshape(8, N, N, CAP) > 0) == there).all(): bad.append("vl and pl name the same slots")
        if not name: bad.append("sn names the variable of each slot")
    except Exception:
        bad.append("shapes")
    return bad
def reference(x, sn, pl, vl):
    g = np.arange(8)[:, None, None]; r = np.arange(N)[:, None]
    ve = np.stack([gentries(vl[p]).astype(np.int64) for p in range(N)], axis=1) + (g * N + r) * N * CAP
    k = np.stack([gentries(pl[q]).astype(np.int64) for q in range(N)], axis=1); p = k // CAP
    ce = (((g - p * r) % 8 * N + p) * N + r) * CAP + k % CAP
    u = x.astype(np.float32).astype(np.int64).reshape(N, 8, 16, V).transpose(2, 1, 0, 3)
    back = np.zeros((16, 8 * N * N * CAP), np.int64); there = np.zeros((16, 8 * N * N * CAP), np.int64); tot = u
    for i in range(IT):
        there[:, ve] = np.clip(np.tile(tot, (1, 1, 1, DV)) - back[:, ve], -B, B)
        m = there[:, ce].reshape(16, 8, N, DC, M); size = np.abs(m); neg = (m < 0).astype(np.int64); new = np.zeros_like(m)
        for e in range(DC):
            o = [j for j in range(DC) if j != e]
            new[:, :, :, e] = np.min(size[:, :, :, o], axis=3) * (1 - 2 * (np.add.reduce(neg[:, :, :, o], axis=3) % 2))
        back[:, ce] = new.reshape(16, 8, N, E)
        tot = u + np.add.reduce(back[:, ve].reshape(16, 8, N, DV, V), axis=3)
    return {"y": np.ascontiguousarray(tot.transpose(2, 1, 0, 3)).reshape(N, 128, V).astype(np.float32)}

@@ -1,0 +1,283 @@
+from concourse.bass import DstId, RemoteDMATransfer
+from concourse.mybir import dt, AluOpType, AxisListType, ActivationFunctionType
+
+NR, CAP, V, M = 8, 160, 256, 128
+W = NR * CAP
+H = W // 2
+NJ = 9 * M
+B = 51.0
+OP = AluOpType
+AF = ActivationFunctionType
+
+SCRATCH = {
+    "sn32": ("sbuf", [128, 80], "int32"), "pl32": ("sbuf", [128, 64], "int32"), "vl32": ("sbuf", [128, 64], "int32"),
+    "sn16": ("sbuf", [128, 80], "uint16"), "pl16": ("sbuf", [128, 64], "uint16"), "vl16": ("sbuf", [128, 64], "uint16"),
+    "ta": ("sbuf", [128, 64], "int32"), "tb": ("sbuf", [128, 64], "int32"), "tc": ("sbuf", [128, 64], "int32"),
+    "td": ("sbuf", [128, 64], "int32"), "pc16": ("sbuf", [128, 64], "uint16"),
+    "num": ("sbuf", [128, 1024], "float32"), "invw": ("sbuf", [128, 1360], "float32"),
+    "invd": ("dram", [8, 17, 1280], "float32"), "inv32": ("sbuf", [128, 80], "float32"), "inv16": ("sbuf", [128, 80], "uint16"),
+    "ei": ("sbuf", [128, 256], "float32"), "E": ("sbuf", [128, 256], "bfloat16"), "NI": ("sbuf", [128, 128], "bfloat16"),
+    "xs": ("sbuf", [128, 256], "bfloat16"), "Tw": ("sbuf", [128, 256], "bfloat16"), "ys": ("sbuf", [128, 256], "float32"),
+    "dwin": ("sbuf", [128, W], "bfloat16"),
+    "D": ("sbuf", [128, NJ], "bfloat16"), "A": ("sbuf", [128, NJ], "bfloat16"), "NA": ("sbuf", [128, NJ], "bfloat16"),
+    "Sg": ("sbuf", [128, NJ], "bfloat16"), "F": ("sbuf", [128, NJ + 16], "bfloat16"), "rst": ("sbuf", [128, NJ], "bfloat16"),
+    "two": ("sbuf", [128, NJ], "bfloat16"),
+    "C0": ("sbuf", [128, 2 * NJ], "bfloat16"), "C1": ("sbuf", [128, 2 * NJ], "bfloat16"), "C2": ("sbuf", [128, 2 * NJ], "bfloat16"),
+    "sc": ("sbuf", [128, H], "bfloat16"), "so": ("sbuf", [128, H], "bfloat16"), "Rf": ("sbuf", [128, H], "bfloat16"),
+    "bk0": ("psum", [128, 512], "float32"), "bk1": ("psum", [128, 512], "float32"),
+    "bk2": ("psum", [128, 512], "float32"), "bk3": ("psum", [128, 512], "float32"),
+    "tt": ("psum", [128, 512], "float32"), "sg0": ("psum", [128, 512], "float32"), "sg1": ("psum", [128, 512], "float32"),
+}
+for _r in range(2):
+    for _n, _w in (("Tg", W), ("Rs", W), ("Lm", W), ("Lr", W), ("Rv", W), ("Gv", 1024), ("sv", H)):
+        SCRATCH["%s%d" % (_n, _r)] = ("sbuf", [128, _w], "bfloat16")
+SEMAPHORES = ["sV", "sA", "sP", "sG", "dx", "dsn", "dpl", "dvl", "dw", "dr", "dy", "ls"]
+SEMAPHORES += ["arr%d_%d" % (ph, p) for ph in range(4) for p in range(NR)]
+
+
+def rank_program(g, core, T, topo):
+    me = T.rank_of(core)
+    if me is None:
+        return
+    queue = {"V": g.vector, "A": g.scalar, "P": g.tensor, "G": g, "S": g.sync}
+    cnt = {"V": 0, "A": 0, "P": 0, "G": 0, "ls": 0}
+    seen = {}
+    vec, act, ten = g.vector, g.scalar, g.tensor
+
+    def need(q, *toks):
+        for sem, val in toks:
+            if seen.get((q, sem), 0) < val:
+                queue[q].wait_ge(T.sem[sem], val)
+                seen[(q, sem)] = val
+
+    def run(q, inst):
+        cnt[q] += 1
+        inst.then_inc(T.sem["s" + q], 1)
+        return ("s" + q, cnt[q])
+
+    h = me // 4
+    o = 1 - h
+
+    def half(buf, k):
+        return buf[:, k * H:(k + 1) * H]
+
+    def blk(buf, q):
+        return buf[:, q * CAP:(q + 1) * CAP]
+
+    def turn(k):
+        s = (128 - 16 * (k % 8)) % 128
+        return T.E[:, s:s + 128]
+
+    eye = T.E[:, 0:128]
+    g.sync.dma_start(T.sn32[:, :], T.sn[:, :]).then_inc(T.sem.dsn, 16)
+    act.dma_start(T.xs[:, :], T.x[:, :]).then_inc(T.sem.dx, 16)
+    g.sync.dma_start(T.pl32[:, :], T.pl[:, :]).then_inc(T.sem.dpl, 16)
+    act.dma_start(T.vl32[:, :], T.vl[:, :]).then_inc(T.sem.dvl, 16)
+    sn_in, x_in, pl_in, vl_in = ("dsn", 16), ("dx", 16), ("dpl", 16), ("dvl", 16)
+    ei = run("G", g.iota(T.ei[:, :], [[0, 2], [1, 128]], 0, -1, allow_small_or_imprecise_dtypes=True))
+    num = run("G", g.iota(T.num[:, :], [[2, 8], [18, 128]], 1, 0, allow_small_or_imprecise_dtypes=True))
+    fill = run("V", vec.memset(T.invw[:, :], 0.0))
+    rst0 = run("V", vec.memset(T.rst[:, :], 0.0))
+    need("V", ei)
+    eyes = run("V", vec.tensor_scalar(T.E[:, :], T.ei[:, :], 0.0, None, OP.is_equal))
+    need("V", sn_in)
+    sn16 = run("V", vec.tensor_copy(T.sn16[:, :], T.sn32[:, :]))
+
+    def send(ph, src, dst, k):
+        dests = [r for r in range(4 * k, 4 * k + 4) if r != me]
+        dests = sorted(dests, key=lambda r: (r - me) % NR)
+        share = [2, 2, 4] if len(dests) == 3 else [2, 2, 2, 2]
+        tr, at = [], 0
+        for r, n in zip(dests, share):
+            c = T.cores[r]
+            rid, pid, _s = topo.addr(c)
+            eng = topo.engines(core, c)[at:at + n]
+            at += n
+            tr.append(RemoteDMATransfer(dst_ids=[DstId(rid=rid, pnc=pid)], dma_engine_mask=sum(1 << e for e in eng),
+                                        remote_sem=T.sem["arr%d_%d" % (ph, me)], src=blk(src, r), dst=blk(dst, me)))
+            cnt["ls"] += n
+        g.remote_dma_fused(tr, local_sem=T.sem.ls)
+
+    def engines_from(p):
+        if p // 4 != h:
+            return 2
+        order = sorted([r for r in range(4 * h, 4 * h + 4) if r != p], key=lambda r: (r - p) % NR)
+        return [2, 2, 4][order.index(me)]
+
+    def var_gather(r, win, ready):
+        dst = T["Tg%d" % r]
+        need("V", sn16, *ready)
+        a = run("V", vec.tensor_copy(half(dst, h), win[:, 0:256].indirect(T.sn16[:, 40 * h:40 * h + 40])))
+        need("A", sn16, *ready)
+        b = run("A", act.activation(half(dst, o), win[:, 0:256].indirect(T.sn16[:, 40 * o:40 * o + 40]), AF.Copy))
+        need("G", a)
+        send(2 * r, dst, T["Lm%d" % r], h)
+        need("G", b)
+        send(2 * r, dst, T["Lm%d" % r], o)
+        return a, b
+
+    tg = var_gather(0, T.xs, [x_in])
+    need("A", tg[1])
+    sv = run("A", act.activation(T.sv0[:, :], half(T.Tg0, o), AF.Sign, bias=0.5))
+    need("V", pl_in)
+    ta = run("V", vec.tensor_scalar(T.ta[:, :], T.pl32[:, :], 15, None, OP.bitwise_and))
+    tb = run("V", vec.tensor_scalar(T.tb[:, :], T.pl32[:, :], 4, None, OP.arith_shift_right))
+    need("V", ta)
+    tc = run("V", vec.tensor_scalar(T.tc[:, :], T.ta[:, :], -80.0, 1280.0, OP.mult, OP.add))
+    need("V", tb, tc)
+    td = run("V", vec.tensor_tensor(T.td[:, :], T.tc[:, :], T.tb[:, :], OP.add))
+    need("V", td)
+    pc = run("V", vec.tensor_copy(T.pc16[:, :], T.td[:, :]))
+    need("V", pc, fill, num)
+    scat = run("V", vec.tensor_copy(T.invw[:, 0:1360].indirect(T.pc16[:, 0:64]), T.num[:, :]))
+    need("S", scat)
+    g.sync.dma_start(T.invd[:, :, :], T.invw[:, :]).then_inc(T.sem.dw, 16)
+    need("S", ("dw", 16))
+    g.sync.dma_start(T.inv32[:, :], T.invd[:, 1:17, 0:80]).then_inc(T.sem.dr, 16)
+    pl16 = run("V", vec.tensor_copy(T.pl16[:, :], T.pl32[:, :]))
+    need("V", vl_in)
+    vl16 = run("V", vec.tensor_copy(T.vl16[:, :], T.vl32[:, :]))
+    need("V", eyes, rst0)
+    ni = run("V", vec.tensor_scalar(T.NI[:, :], eye, -1.0, None, OP.mult))
+    run("V", vec.memset(T.rst[:, 0:NJ:9], B))
+    run("V", vec.memset(T.two[:, :], 2.0))
+    run("V", vec.memset(T.D[:, 8:NJ:9], 1.0))
+    run("V", vec.memset(T.F[:, 7:8], 8.0))
+    run("V", vec.memset(T.C0[:, 0:2 * NJ:2], 64.0))
+    run("V", vec.memset(T.C1[:, 1:2], B))
+    consts = run("V", vec.memset(T.C1[:, 2 * NJ - 2:2 * NJ - 1], 0.0))
+
+    def order():
+        first = [me, me ^ 1] + [4 * h + (2 - 2 * (me % 4 // 2)) + i for i in range(2)]
+        return first + [4 * o + i for i in range(4)]
+
+    def turned(ph, mine, mine_ready, land, way, minus):
+        done = {}
+        need("P", eyes, ni)
+        if minus is not None:
+            need("P", rf[0])
+        for p in order():
+            bank = T["bk%d" % (p // 2)]
+            out = bank[:, (p % 2) * CAP:(p % 2 + 1) * CAP]
+            if p == me:
+                need("P", *mine_ready)
+                src = blk(mine, p)
+            else:
+                need("P", ("arr%d_%d" % (ph, p), engines_from(p)))
+                src = blk(land, p)
+            k = way * me * p
+            run_tok = run("P", ten.matmul(out, turn(k), src, True, minus is None))
+            if minus is not None:
+                run_tok = run("P", ten.matmul(out, T.NI[:, :], minus(p), False, True))
+            done[p // 2] = run_tok
+        return done
+
+    def bank_order(k):
+        return [me // 2, (me // 2) ^ 1] if k == h else [2 * k, 2 * k + 1]
+
+    def check(r, tg):
+        done = turned(2 * r, T["Tg%d" % r], tg, T["Lm%d" % r], 1, own_r if r else None)
+        ev = []
+        for q, k in (("V", h), ("A", o)):
+            for b in bank_order(k):
+                need(q, done[b])
+                dst, src = T.dwin[:, 320 * b:320 * b + 320], T["bk%d" % b][:, 0:320]
+                inst = vec.tensor_copy(dst, src) if q == "V" else act.activation(dst, src, AF.Copy)
+                ev.append(run(q, inst))
+        win = T.dwin[:, 0:W]
+        need("V", pl16, *ev)
+        need("A", pl16, *ev)
+        for e in range(4):
+            gv = run("V", vec.tensor_copy(T.D[:, e:NJ:9], win.indirect(T.pl16[:, 8 * e:8 * e + 8])))
+            ga = run("A", act.activation(T.D[:, e + 4:NJ:9], win.indirect(T.pl16[:, 8 * e + 32:8 * e + 40]), AF.Copy))
+        need("V", gv, ga, consts)
+        need("A", gv, ga, consts)
+        sg = run("V", vec.tensor_scalar(T.Sg[:, :], T.D[:, :], 0.0, -0.5, OP.is_ge, OP.add))
+        ab = run("A", act.activation(T.A[:, :], T.D[:, :], AF.Abs))
+        need("V", sg)
+        f = run("V", vec.tensor_tensor_scan(T.F[:, 9:9 + NJ], T.Sg[:, :], T.two[:, :], 8.0, OP.mult, OP.mult))
+        need("A", ab)
+        na = run("A", act.activation(T.NA[:, :], T.A[:, :], AF.Copy, scale=-1.0))
+        sc = run("A", act.activation(T.sc[:, :], half(T.dwin, h), AF.Sign, bias=0.5))
+        need("V", ab)
+        pre = run("V", vec.tensor_tensor_scan(T.C1[:, 3:2 * NJ:2], T.A[:, 0:NJ - 1], T.rst[:, 1:NJ], B, OP.min, OP.max))
+        need("V", pre)
+        neg = run("V", vec.tensor_scalar(T.C0[:, 1:2 * NJ:2], T.C1[:, 1:2 * NJ:2], -1.0, None, OP.mult))
+        need("V", na, f)
+        su = run("V", vec.tensor_tensor(T.A[:, 8:NJ:9], T.F[:, 16:NJ + 9:9], T.F[:, 7:NJ:9], OP.mult))
+        nu = run("V", vec.memset(T.NA[:, 8:NJ:9], 64.0))
+        need("V", su, nu)
+        suf = run("V", vec.tensor_tensor_scan(T.C1[:, 2 * NJ - 4::-2], T.NA[:, NJ - 1:0:-1], T.A[:, NJ - 1:0:-1], 0.0, OP.max, OP.min))
+        if r == 0:
+            need("V", ("dr", 16))
+            inv[0] = run("V", vec.tensor_copy(T.inv16[:, :], T.inv32[:, :]))
+        need("V", suf, neg)
+        w = run("V", vec.tensor_tensor_scan(T.C2[:, :], T.C0[:, :], T.C1[:, :], 0.0, OP.max, OP.min))
+        dst = T["Rs%d" % r]
+        need("V", w, sc, inv[0])
+        a = run("V", vec.tensor_tensor(half(dst, h), T.C2[:, 0:2 * NJ].indirect(T.inv16[:, 40 * h:40 * h + 40]), T.sc[:, :], OP.mult))
+        need("A", w, inv[0])
+        b = run("A", act.activation(half(dst, o), T.C2[:, 0:2 * NJ].indirect(T.inv16[:, 40 * o:40 * o + 40]), AF.Copy))
+        need("G", a)
+        send(2 * r + 1, dst, T["Lr%d" % r], h)
+        need("G", b)
+        send(2 * r + 1, dst, T["Lr%d" % r], o)
+        if r == 0:
+            so = run("A", act.activation(T.so[:, :], half(T.dwin, o), AF.Sign, bias=0.5))
+            need("V", so, b)
+            rf[0] = run("V", vec.tensor_tensor(T.Rf[:, :], half(dst, o), T.so[:, :], OP.mult))
+        return [a]
+
+    def variables(r, rs, sv):
+        done = turned(2 * r + 1, T["Rs%d" % r], rs, T["Lr%d" % r], -1, None)
+        rv, ev = T["Rv%d" % r], []
+        for q, k in (("A", h), ("V", o)):
+            for b in bank_order(k):
+                need(q, done[b])
+                dst, src = rv[:, 320 * b:320 * b + 320], T["bk%d" % b][:, 0:320]
+                if q == "A":
+                    inst = act.activation(dst, src, AF.Copy)
+                else:
+                    need("V", *sv)
+                    i = b - 2 * o
+                    inst = vec.tensor_tensor(dst, src, T["sv%d" % r][:, 320 * i:320 * i + 320], OP.mult)
+                ev.append(run(q, inst))
+        gd = T["Gv%d" % r]
+        need("V", vl16, *ev)
+        a = run("V", vec.tensor_copy(gd[:, 0:512], rv[:, 0:W].indirect(T.vl16[:, 0:32])))
+        need("A", vl16, *ev)
+        b = run("A", act.activation(gd[:, 512:1024], rv[:, 0:W].indirect(T.vl16[:, 32:64]), AF.Copy))
+        need("P", x_in)
+        run("P", ten.matmul(T.tt[:, 0:256], eye, T.xs[:, :], True, False))
+        need("P", a)
+        for d in range(2):
+            run("P", ten.matmul(T.tt[:, 0:256], eye, gd[:, 256 * d:256 * d + 256], False, False))
+        need("P", b)
+        for d in range(2, 4):
+            t = run("P", ten.matmul(T.tt[:, 0:256], eye, gd[:, 256 * d:256 * d + 256], False, d == 3))
+        need("V", t)
+
+    def own_r(p):
+        return blk(T.Rs0, p) if p // 4 == h else blk(T.Rf, p - 4 * o)
+
+    inv, rf = [None], [None]
+    rs = check(0, [tg[0]])
+    variables(0, rs, [sv])
+    tw = run("V", vec.tensor_copy(T.Tw[:, :], T.tt[:, 0:256]))
+    tg = var_gather(1, T.Tw, [tw])
+    need("P", tg[1])
+    for i in range(2):
+        cols = slice(o * H + 320 * i, o * H + 320 * i + 320)
+        run("P", ten.matmul(T["sg%d" % i][:, 0:320], eye, T.Tg1[:, cols], True, False))
+        t = run("P", ten.matmul(T["sg%d" % i][:, 0:320], T.NI[:, :], T.Rv0[:, cols], False, True))
+        need("A", t)
+        sv = run("A", act.activation(T.sv1[:, 320 * i:320 * i + 320], T["sg%d" % i][:, 0:320], AF.Sign, bias=0.5))
+    rs = check(1, [tg[0]])
+    variables(1, rs, [sv])
+    yt = run("V", vec.tensor_copy(T.ys[:, :], T.tt[:, 0:256]))
+    need("S", yt)
+    g.sync.dma_start(T.y[:, :], T.ys[:, :]).then_inc(T.sem.dy, 16)
+    need("S", ("dy", 16))
+    for q in ("V", "A", "P", "G"):
+        need("G", ("s" + q, cnt[q]))
+    need("G", ("ls", cnt["ls"]))

@@ -3,8 +3,10 @@ from concourse.mybir import dt, AluOpType, AxisListType, ActivationFunctionType
 
 NR, CAP, V, M = 8, 160, 256, 128
 W = NR * CAP
-H = W // 2
+BK = 2 * CAP
+H = 2 * BK
 NJ = 9 * M
+NH = NJ // 2
 B = 51.0
 OP = AluOpType
 AF = ActivationFunctionType
@@ -20,8 +22,7 @@ SCRATCH = {
     "xs": ("sbuf", [128, 256], "bfloat16"), "Tw": ("sbuf", [128, 256], "bfloat16"), "ys": ("sbuf", [128, 256], "float32"),
     "dwin": ("sbuf", [128, W], "bfloat16"),
     "D": ("sbuf", [128, NJ], "bfloat16"), "A": ("sbuf", [128, NJ], "bfloat16"), "NA": ("sbuf", [128, NJ], "bfloat16"),
-    "Sg": ("sbuf", [128, NJ], "bfloat16"), "F": ("sbuf", [128, NJ + 16], "bfloat16"), "rst": ("sbuf", [128, NJ], "bfloat16"),
-    "two": ("sbuf", [128, NJ], "bfloat16"),
+    "F": ("sbuf", [128, NJ], "bfloat16"), "rst": ("sbuf", [128, NJ], "bfloat16"), "inj": ("sbuf", [128, NJ], "bfloat16"),
     "C0": ("sbuf", [128, 2 * NJ], "bfloat16"), "C1": ("sbuf", [128, 2 * NJ], "bfloat16"), "C2": ("sbuf", [128, 2 * NJ], "bfloat16"),
     "sc": ("sbuf", [128, H], "bfloat16"), "so": ("sbuf", [128, H], "bfloat16"), "Rf": ("sbuf", [128, H], "bfloat16"),
     "bk0": ("psum", [128, 512], "float32"), "bk1": ("psum", [128, 512], "float32"),
@@ -56,10 +57,12 @@ def rank_program(g, core, T, topo):
         return ("s" + q, cnt[q])
 
     h = me // 4
-    o = 1 - h
+    s0 = me // 2
+    same = [s0, s0 ^ 2]
+    diff = [s0 ^ 1, s0 ^ 3]
 
-    def half(buf, k):
-        return buf[:, k * H:(k + 1) * H]
+    def bank(buf, b):
+        return buf[:, b * BK:(b + 1) * BK]
 
     def blk(buf, q):
         return buf[:, q * CAP:(q + 1) * CAP]
@@ -77,18 +80,20 @@ def rank_program(g, core, T, topo):
     ei = run("G", g.iota(T.ei[:, :], [[0, 2], [1, 128]], 0, -1, allow_small_or_imprecise_dtypes=True))
     num = run("G", g.iota(T.num[:, :], [[2, 8], [18, 128]], 1, 0, allow_small_or_imprecise_dtypes=True))
     fill = run("V", vec.memset(T.invw[:, :], 0.0))
-    rst0 = run("V", vec.memset(T.rst[:, :], 0.0))
+    run("V", vec.memset(T.rst[:, :], 0.0))
+    zeros = run("V", vec.memset(T.inj[:, :], 0.0))
     need("V", ei)
     eyes = run("V", vec.tensor_scalar(T.E[:, :], T.ei[:, :], 0.0, None, OP.is_equal))
     need("V", sn_in)
     sn16 = run("V", vec.tensor_copy(T.sn16[:, :], T.sn32[:, :]))
 
+    def dests_of(p, k):
+        d = sorted([r for r in range(4 * k, 4 * k + 4) if r != p], key=lambda r: (r - p) % NR)
+        return list(zip(d, [2, 2, 4] if len(d) == 3 else [2, 2, 2, 2]))
+
     def send(ph, src, dst, k):
-        dests = [r for r in range(4 * k, 4 * k + 4) if r != me]
-        dests = sorted(dests, key=lambda r: (r - me) % NR)
-        share = [2, 2, 4] if len(dests) == 3 else [2, 2, 2, 2]
         tr, at = [], 0
-        for r, n in zip(dests, share):
+        for r, n in dests_of(me, k):
             c = T.cores[r]
             rid, pid, _s = topo.addr(c)
             eng = topo.engines(core, c)[at:at + n]
@@ -98,27 +103,24 @@ def rank_program(g, core, T, topo):
             cnt["ls"] += n
         g.remote_dma_fused(tr, local_sem=T.sem.ls)
 
-    def engines_from(p):
-        if p // 4 != h:
-            return 2
-        order = sorted([r for r in range(4 * h, 4 * h + 4) if r != p], key=lambda r: (r - p) % NR)
-        return [2, 2, 4][order.index(me)]
-
     def var_gather(r, win, ready):
         dst = T["Tg%d" % r]
         need("V", sn16, *ready)
-        a = run("V", vec.tensor_copy(half(dst, h), win[:, 0:256].indirect(T.sn16[:, 40 * h:40 * h + 40])))
         need("A", sn16, *ready)
-        b = run("A", act.activation(half(dst, o), win[:, 0:256].indirect(T.sn16[:, 40 * o:40 * o + 40]), AF.Copy))
-        need("G", a)
-        send(2 * r, dst, T["Lm%d" % r], h)
-        need("G", b)
-        send(2 * r, dst, T["Lm%d" % r], o)
+        a, b = [], []
+        for i in range(2):
+            s, d = same[i], diff[i]
+            a.append(run("V", vec.tensor_copy(bank(dst, s), win[:, 0:256].indirect(T.sn16[:, 20 * s:20 * s + 20]))))
+            b.append(run("A", act.activation(bank(dst, d), win[:, 0:256].indirect(T.sn16[:, 20 * d:20 * d + 20]), AF.Copy)))
+        for i in range(2):
+            need("G", a[i], b[i])
+            send(2 * r, dst, T["Lm%d" % r], h if i == 0 else 1 - h)
         return a, b
 
     tg = var_gather(0, T.xs, [x_in])
-    need("A", tg[1])
-    sv = run("A", act.activation(T.sv0[:, :], half(T.Tg0, o), AF.Sign, bias=0.5))
+    need("A", tg[1][1])
+    for i in range(2):
+        sv = run("A", act.activation(bank(T.sv0, i), bank(T.Tg0, diff[i]), AF.Sign, bias=0.5))
     need("V", pl_in)
     ta = run("V", vec.tensor_scalar(T.ta[:, :], T.pl32[:, :], 15, None, OP.bitwise_and))
     tb = run("V", vec.tensor_scalar(T.tb[:, :], T.pl32[:, :], 4, None, OP.arith_shift_right))
@@ -137,53 +139,44 @@ def rank_program(g, core, T, topo):
     pl16 = run("V", vec.tensor_copy(T.pl16[:, :], T.pl32[:, :]))
     need("V", vl_in)
     vl16 = run("V", vec.tensor_copy(T.vl16[:, :], T.vl32[:, :]))
-    need("V", eyes, rst0)
+    need("V", eyes, zeros)
     ni = run("V", vec.tensor_scalar(T.NI[:, :], eye, -1.0, None, OP.mult))
     run("V", vec.memset(T.rst[:, 0:NJ:9], B))
-    run("V", vec.memset(T.two[:, :], 2.0))
-    run("V", vec.memset(T.D[:, 8:NJ:9], 1.0))
-    run("V", vec.memset(T.F[:, 7:8], 8.0))
+    run("V", vec.memset(T.inj[:, 8:NJ:9], 16384.0))
+    run("V", vec.memset(T.D[:, 8:NJ:9], 0.0))
     run("V", vec.memset(T.C0[:, 0:2 * NJ:2], 64.0))
     run("V", vec.memset(T.C1[:, 1:2], B))
     consts = run("V", vec.memset(T.C1[:, 2 * NJ - 2:2 * NJ - 1], 0.0))
-
-    def order():
-        first = [me, me ^ 1] + [4 * h + (2 - 2 * (me % 4 // 2)) + i for i in range(2)]
-        return first + [4 * o + i for i in range(4)]
 
     def turned(ph, mine, mine_ready, land, way, minus):
         done = {}
         need("P", eyes, ni)
         if minus is not None:
             need("P", rf[0])
-        for p in order():
-            bank = T["bk%d" % (p // 2)]
-            out = bank[:, (p % 2) * CAP:(p % 2 + 1) * CAP]
+        for p in [me, me ^ 1] + [2 * b + i for b in (diff[0], same[1], diff[1]) for i in range(2)]:
+            out = blk(T["bk%d" % (p // 2)], p % 2)
             if p == me:
-                need("P", *mine_ready)
+                need("P", mine_ready)
                 src = blk(mine, p)
             else:
-                need("P", ("arr%d_%d" % (ph, p), engines_from(p)))
+                need("P", ("arr%d_%d" % (ph, p), dict(dests_of(p, h))[me]))
                 src = blk(land, p)
-            k = way * me * p
-            run_tok = run("P", ten.matmul(out, turn(k), src, True, minus is None))
+            tok = run("P", ten.matmul(out, turn(way * me * p), src, True, minus is None))
             if minus is not None:
-                run_tok = run("P", ten.matmul(out, T.NI[:, :], minus(p), False, True))
-            done[p // 2] = run_tok
+                tok = run("P", ten.matmul(out, T.NI[:, :], minus(p), False, True))
+            done[p // 2] = tok
         return done
 
-    def bank_order(k):
-        return [me // 2, (me // 2) ^ 1] if k == h else [2 * k, 2 * k + 1]
-
-    def check(r, tg):
-        done = turned(2 * r, T["Tg%d" % r], tg, T["Lm%d" % r], 1, own_r if r else None)
+    def check(r, mine_ready):
+        done = turned(2 * r, T["Tg%d" % r], mine_ready, T["Lm%d" % r], 1, own_r if r else None)
         ev = []
-        for q, k in (("V", h), ("A", o)):
-            for b in bank_order(k):
-                need(q, done[b])
-                dst, src = T.dwin[:, 320 * b:320 * b + 320], T["bk%d" % b][:, 0:320]
-                inst = vec.tensor_copy(dst, src) if q == "V" else act.activation(dst, src, AF.Copy)
-                ev.append(run(q, inst))
+        for i in range(2):
+            b = same[i]
+            need("V", done[b])
+            ev.append(run("V", vec.tensor_scalar(bank(T.dwin, b), bank(T["bk%d" % b], 0), 0.5, None, OP.add)))
+            b = diff[i]
+            need("A", done[b])
+            ev.append(run("A", act.activation(bank(T.dwin, b), bank(T["bk%d" % b], 0), AF.Identity, bias=0.5)))
         win = T.dwin[:, 0:W]
         need("V", pl16, *ev)
         need("A", pl16, *ev)
@@ -192,21 +185,22 @@ def rank_program(g, core, T, topo):
             ga = run("A", act.activation(T.D[:, e + 4:NJ:9], win.indirect(T.pl16[:, 8 * e + 32:8 * e + 40]), AF.Copy))
         need("V", gv, ga, consts)
         need("A", gv, ga, consts)
-        sg = run("V", vec.tensor_scalar(T.Sg[:, :], T.D[:, :], 0.0, -0.5, OP.is_ge, OP.add))
-        ab = run("A", act.activation(T.A[:, :], T.D[:, :], AF.Abs))
-        need("V", sg)
-        f = run("V", vec.tensor_tensor_scan(T.F[:, 9:9 + NJ], T.Sg[:, :], T.two[:, :], 8.0, OP.mult, OP.mult))
-        need("A", ab)
-        na = run("A", act.activation(T.NA[:, :], T.A[:, :], AF.Copy, scale=-1.0))
-        sc = run("A", act.activation(T.sc[:, :], half(T.dwin, h), AF.Sign, bias=0.5))
-        need("V", ab)
-        pre = run("V", vec.tensor_tensor_scan(T.C1[:, 3:2 * NJ:2], T.A[:, 0:NJ - 1], T.rst[:, 1:NJ], B, OP.min, OP.max))
-        need("V", pre)
-        neg = run("V", vec.tensor_scalar(T.C0[:, 1:2 * NJ:2], T.C1[:, 1:2 * NJ:2], -1.0, None, OP.mult))
-        need("V", na, f)
-        su = run("V", vec.tensor_tensor(T.A[:, 8:NJ:9], T.F[:, 16:NJ + 9:9], T.F[:, 7:NJ:9], OP.mult))
+        f = run("V", vec.tensor_tensor_scan(T.F[:, :], T.D[:, :], T.inj[:, :], 16384.0, OP.mult, OP.add))
+        ab = [run("A", act.activation(T.A[:, k * NH:(k + 1) * NH], T.D[:, k * NH:(k + 1) * NH], AF.Abs, bias=-0.5)) for k in range(2)]
+        for k in range(2):
+            need("V", ab[k])
+            lo, hi = (1, NH + 1) if k == 0 else (NH + 1, NJ)
+            pre = run("V", vec.tensor_tensor_scan(T.C1[:, 2 * lo + 1:2 * hi:2], T.A[:, lo - 1:hi - 1], T.rst[:, lo:hi], B, OP.min, OP.max))
+            na = run("V", vec.tensor_scalar(T.NA[:, k * NH:(k + 1) * NH], T.A[:, k * NH:(k + 1) * NH], -1.0, None, OP.mult))
+            need("A", pre)
+            lo = lo - 1 if k == 0 else lo
+            neg = run("A", act.activation(T.C0[:, 2 * lo + 1:2 * hi:2], T.C1[:, 2 * lo + 1:2 * hi:2], AF.Copy, scale=-1.0))
+        for i in range(2):
+            sc = run("A", act.activation(bank(T.sc, i), bank(T.dwin, same[i]), AF.Sign))
+        need("V", f, na)
+        run("V", vec.tensor_copy(T.A[:, 8:NJ:9], T.F[:, 7:NJ:9]))
         nu = run("V", vec.memset(T.NA[:, 8:NJ:9], 64.0))
-        need("V", su, nu)
+        need("V", nu)
         suf = run("V", vec.tensor_tensor_scan(T.C1[:, 2 * NJ - 4::-2], T.NA[:, NJ - 1:0:-1], T.A[:, NJ - 1:0:-1], 0.0, OP.max, OP.min))
         if r == 0:
             need("V", ("dr", 16))
@@ -215,37 +209,39 @@ def rank_program(g, core, T, topo):
         w = run("V", vec.tensor_tensor_scan(T.C2[:, :], T.C0[:, :], T.C1[:, :], 0.0, OP.max, OP.min))
         dst = T["Rs%d" % r]
         need("V", w, sc, inv[0])
-        a = run("V", vec.tensor_tensor(half(dst, h), T.C2[:, 0:2 * NJ].indirect(T.inv16[:, 40 * h:40 * h + 40]), T.sc[:, :], OP.mult))
         need("A", w, inv[0])
-        b = run("A", act.activation(half(dst, o), T.C2[:, 0:2 * NJ].indirect(T.inv16[:, 40 * o:40 * o + 40]), AF.Copy))
-        need("G", a)
-        send(2 * r + 1, dst, T["Lr%d" % r], h)
-        need("G", b)
-        send(2 * r + 1, dst, T["Lr%d" % r], o)
+        win = T.C2[:, 0:2 * NJ]
+        a, b = [], []
+        for i in range(2):
+            s, d = same[i], diff[i]
+            a.append(run("V", vec.tensor_tensor(bank(dst, s), win.indirect(T.inv16[:, 20 * s:20 * s + 20]), bank(T.sc, i), OP.mult)))
+            b.append(run("A", act.activation(bank(dst, d), win.indirect(T.inv16[:, 20 * d:20 * d + 20]), AF.Copy)))
+        for i in range(2):
+            need("G", a[i], b[i])
+            send(2 * r + 1, dst, T["Lr%d" % r], h if i == 0 else 1 - h)
         if r == 0:
-            so = run("A", act.activation(T.so[:, :], half(T.dwin, o), AF.Sign, bias=0.5))
-            need("V", so, b)
-            rf[0] = run("V", vec.tensor_tensor(T.Rf[:, :], half(dst, o), T.so[:, :], OP.mult))
-        return [a]
+            for i in range(2):
+                so = run("A", act.activation(bank(T.so, i), bank(T.dwin, diff[i]), AF.Sign))
+            need("V", so, b[1])
+            for i in range(2):
+                rf[0] = run("V", vec.tensor_tensor(bank(T.Rf, i), bank(dst, diff[i]), bank(T.so, i), OP.mult))
+        return a[0]
 
     def variables(r, rs, sv):
         done = turned(2 * r + 1, T["Rs%d" % r], rs, T["Lr%d" % r], -1, None)
         rv, ev = T["Rv%d" % r], []
-        for q, k in (("A", h), ("V", o)):
-            for b in bank_order(k):
-                need(q, done[b])
-                dst, src = rv[:, 320 * b:320 * b + 320], T["bk%d" % b][:, 0:320]
-                if q == "A":
-                    inst = act.activation(dst, src, AF.Copy)
-                else:
-                    need("V", *sv)
-                    i = b - 2 * o
-                    inst = vec.tensor_tensor(dst, src, T["sv%d" % r][:, 320 * i:320 * i + 320], OP.mult)
-                ev.append(run(q, inst))
+        need("V", sv)
+        for i in range(2):
+            b = same[i]
+            need("A", done[b])
+            ev.append(run("A", act.activation(bank(rv, b), bank(T["bk%d" % b], 0), AF.Copy)))
+            b = diff[i]
+            need("V", done[b])
+            ev.append(run("V", vec.tensor_tensor(bank(rv, b), bank(T["bk%d" % b], 0), bank(T["sv%d" % r], i), OP.mult)))
         gd = T["Gv%d" % r]
         need("V", vl16, *ev)
-        a = run("V", vec.tensor_copy(gd[:, 0:512], rv[:, 0:W].indirect(T.vl16[:, 0:32])))
         need("A", vl16, *ev)
+        a = run("V", vec.tensor_copy(gd[:, 0:512], rv[:, 0:W].indirect(T.vl16[:, 0:32])))
         b = run("A", act.activation(gd[:, 512:1024], rv[:, 0:W].indirect(T.vl16[:, 32:64]), AF.Copy))
         need("P", x_in)
         run("P", ten.matmul(T.tt[:, 0:256], eye, T.xs[:, :], True, False))
@@ -258,22 +254,22 @@ def rank_program(g, core, T, topo):
         need("V", t)
 
     def own_r(p):
-        return blk(T.Rs0, p) if p // 4 == h else blk(T.Rf, p - 4 * o)
+        b = p // 2
+        return blk(T.Rs0, p) if b in same else blk(T.Rf, 2 * diff.index(b) + p % 2)
 
     inv, rf = [None], [None]
-    rs = check(0, [tg[0]])
-    variables(0, rs, [sv])
+    rs = check(0, tg[0][0])
+    variables(0, rs, sv)
     tw = run("V", vec.tensor_copy(T.Tw[:, :], T.tt[:, 0:256]))
     tg = var_gather(1, T.Tw, [tw])
-    need("P", tg[1])
+    need("P", tg[1][1])
     for i in range(2):
-        cols = slice(o * H + 320 * i, o * H + 320 * i + 320)
-        run("P", ten.matmul(T["sg%d" % i][:, 0:320], eye, T.Tg1[:, cols], True, False))
-        t = run("P", ten.matmul(T["sg%d" % i][:, 0:320], T.NI[:, :], T.Rv0[:, cols], False, True))
+        run("P", ten.matmul(bank(T["sg%d" % i], 0), eye, bank(T.Tg1, diff[i]), True, False))
+        t = run("P", ten.matmul(bank(T["sg%d" % i], 0), T.NI[:, :], bank(T.Rv0, diff[i]), False, True))
         need("A", t)
-        sv = run("A", act.activation(T.sv1[:, 320 * i:320 * i + 320], T["sg%d" % i][:, 0:320], AF.Sign, bias=0.5))
-    rs = check(1, [tg[0]])
-    variables(1, rs, [sv])
+        sv = run("A", act.activation(bank(T.sv1, i), bank(T["sg%d" % i], 0), AF.Sign, bias=0.5))
+    rs = check(1, tg[0][0])
+    variables(1, rs, sv)
     yt = run("V", vec.tensor_copy(T.ys[:, :], T.tt[:, 0:256]))
     need("S", yt)
     g.sync.dma_start(T.y[:, :], T.ys[:, :]).then_inc(T.sem.dy, 16)

@@ -16,23 +16,24 @@ SCRATCH = {
     "sn16": ("sbuf", [128, 80], "uint16"), "pl16": ("sbuf", [128, 64], "uint16"), "vl16": ("sbuf", [128, 64], "uint16"),
     "ta": ("sbuf", [128, 64], "int32"), "tb": ("sbuf", [128, 64], "int32"), "tc": ("sbuf", [128, 64], "int32"),
     "td": ("sbuf", [128, 64], "int32"), "pc16": ("sbuf", [128, 64], "uint16"),
-    "num": ("sbuf", [128, 1024], "float32"), "invw": ("sbuf", [128, 1360], "float32"),
-    "invd": ("dram", [8, 17, 1280], "float32"), "inv32": ("sbuf", [128, 80], "float32"), "inv16": ("sbuf", [128, 80], "uint16"),
+    "num": ("sbuf", [128, 1024], "float32"), "invw": ("sbuf", [128, W], "float32"),
+    "inv32": ("sbuf", [128, 80], "float32"), "inv16": ("sbuf", [128, 80], "uint16"),
     "ei": ("sbuf", [128, 256], "float32"), "E": ("sbuf", [128, 256], "bfloat16"), "NI": ("sbuf", [128, 128], "bfloat16"),
     "xs": ("sbuf", [128, 256], "bfloat16"), "Tw": ("sbuf", [128, 256], "bfloat16"), "ys": ("sbuf", [128, 256], "float32"),
-    "dwin": ("sbuf", [128, W], "bfloat16"),
+    "dwin": ("sbuf", [128, W], "bfloat16"), "zer": ("sbuf", [128, NJ], "bfloat16"),
     "D": ("sbuf", [128, NJ], "bfloat16"), "A": ("sbuf", [128, NJ], "bfloat16"), "NA": ("sbuf", [128, NJ], "bfloat16"),
     "F": ("sbuf", [128, NJ], "bfloat16"), "rst": ("sbuf", [128, NJ], "bfloat16"), "inj": ("sbuf", [128, NJ], "bfloat16"),
     "C0": ("sbuf", [128, 2 * NJ], "bfloat16"), "C1": ("sbuf", [128, 2 * NJ], "bfloat16"), "C2": ("sbuf", [128, 2 * NJ], "bfloat16"),
     "sc": ("sbuf", [128, H], "bfloat16"), "so": ("sbuf", [128, H], "bfloat16"), "Rf": ("sbuf", [128, H], "bfloat16"),
     "bk0": ("psum", [128, 512], "float32"), "bk1": ("psum", [128, 512], "float32"),
     "bk2": ("psum", [128, 512], "float32"), "bk3": ("psum", [128, 512], "float32"),
-    "tt": ("psum", [128, 512], "float32"), "sg0": ("psum", [128, 512], "float32"), "sg1": ("psum", [128, 512], "float32"),
+    "tt0": ("psum", [128, 512], "float32"), "tt1": ("psum", [128, 512], "float32"),
+    "sg0": ("psum", [128, 512], "float32"), "sg1": ("psum", [128, 512], "float32"),
 }
 for _r in range(2):
     for _n, _w in (("Tg", W), ("Rs", W), ("Lm", W), ("Lr", W), ("Rv", W), ("Gv", 1024), ("sv", H)):
         SCRATCH["%s%d" % (_n, _r)] = ("sbuf", [128, _w], "bfloat16")
-SEMAPHORES = ["sV", "sA", "sP", "sG", "dx", "dsn", "dpl", "dvl", "dw", "dr", "dy", "ls"]
+SEMAPHORES = ["sV", "sA", "sP", "sG", "dx", "dsn", "dpl", "dvl", "dr", "dy", "ls"]
 SEMAPHORES += ["arr%d_%d" % (ph, p) for ph in range(4) for p in range(NR)]
 
 
@@ -77,13 +78,13 @@ def rank_program(g, core, T, topo):
     g.sync.dma_start(T.pl32[:, :], T.pl[:, :]).then_inc(T.sem.dpl, 16)
     act.dma_start(T.vl32[:, :], T.vl[:, :]).then_inc(T.sem.dvl, 16)
     sn_in, x_in, pl_in, vl_in = ("dsn", 16), ("dx", 16), ("dpl", 16), ("dvl", 16)
+    base = run("G", g.iota(T.num[:, 0:128], [[18, 128]], 1, 0, allow_small_or_imprecise_dtypes=True))
     ei = run("G", g.iota(T.ei[:, :], [[0, 2], [1, 128]], 0, -1, allow_small_or_imprecise_dtypes=True))
-    num = run("G", g.iota(T.num[:, :], [[2, 8], [18, 128]], 1, 0, allow_small_or_imprecise_dtypes=True))
+    need("A", base)
+    for e in range(1, 8):
+        num = run("A", act.activation(T.num[:, 128 * e:128 * e + 128], T.num[:, 0:128], AF.Identity, bias=2.0 * e))
     fill = run("V", vec.memset(T.invw[:, :], 0.0))
-    run("V", vec.memset(T.rst[:, :], 0.0))
-    zeros = run("V", vec.memset(T.inj[:, :], 0.0))
-    need("V", ei)
-    eyes = run("V", vec.tensor_scalar(T.E[:, :], T.ei[:, :], 0.0, None, OP.is_equal))
+    zeros = run("V", vec.memset(T.zer[:, :], 0.0))
     need("V", sn_in)
     sn16 = run("V", vec.tensor_copy(T.sn16[:, :], T.sn32[:, :]))
 
@@ -118,35 +119,39 @@ def rank_program(g, core, T, topo):
         return a, b
 
     tg = var_gather(0, T.xs, [x_in])
-    need("A", tg[1][1])
-    for i in range(2):
-        sv = run("A", act.activation(bank(T.sv0, i), bank(T.Tg0, diff[i]), AF.Sign, bias=0.5))
     need("V", pl_in)
     ta = run("V", vec.tensor_scalar(T.ta[:, :], T.pl32[:, :], 15, None, OP.bitwise_and))
     tb = run("V", vec.tensor_scalar(T.tb[:, :], T.pl32[:, :], 4, None, OP.arith_shift_right))
     need("V", ta)
-    tc = run("V", vec.tensor_scalar(T.tc[:, :], T.ta[:, :], -80.0, 1280.0, OP.mult, OP.add))
+    tc = run("V", vec.tensor_scalar(T.tc[:, :], T.ta[:, :], 80.0, None, OP.mult))
     need("V", tb, tc)
     td = run("V", vec.tensor_tensor(T.td[:, :], T.tc[:, :], T.tb[:, :], OP.add))
+    need("V", ei)
+    eyes = run("V", vec.tensor_scalar(T.E[:, :], T.ei[:, :], 0.0, None, OP.is_equal))
     need("V", td)
     pc = run("V", vec.tensor_copy(T.pc16[:, :], T.td[:, :]))
-    need("V", pc, fill, num)
-    scat = run("V", vec.tensor_copy(T.invw[:, 0:1360].indirect(T.pc16[:, 0:64]), T.num[:, :]))
-    need("S", scat)
-    g.sync.dma_start(T.invd[:, :, :], T.invw[:, :]).then_inc(T.sem.dw, 16)
-    need("S", ("dw", 16))
-    g.sync.dma_start(T.inv32[:, :], T.invd[:, 1:17, 0:80]).then_inc(T.sem.dr, 16)
     pl16 = run("V", vec.tensor_copy(T.pl16[:, :], T.pl32[:, :]))
+    need("V", pc, fill, num)
+    scat = run("V", vec.tensor_copy(T.invw[:, 0:W].indirect(T.pc16[:, 0:64]), T.num[:, :]))
+    need("S", scat)
+    g.sync.dma_start(T.inv32[:, :], T.invw[0:128:16, :]).then_inc(T.sem.dr, 16)
+    need("V", eyes)
+    ni = run("V", vec.tensor_scalar(T.NI[:, :], eye, -1.0, None, OP.mult))
     need("V", vl_in)
     vl16 = run("V", vec.tensor_copy(T.vl16[:, :], T.vl32[:, :]))
-    need("V", eyes, zeros)
-    ni = run("V", vec.tensor_scalar(T.NI[:, :], eye, -1.0, None, OP.mult))
-    run("V", vec.memset(T.rst[:, 0:NJ:9], B))
-    run("V", vec.memset(T.inj[:, 8:NJ:9], 16384.0))
-    run("V", vec.memset(T.D[:, 8:NJ:9], 0.0))
-    run("V", vec.memset(T.C0[:, 0:2 * NJ:2], 64.0))
-    run("V", vec.memset(T.C1[:, 1:2], B))
-    consts = run("V", vec.memset(T.C1[:, 2 * NJ - 2:2 * NJ - 1], 0.0))
+    need("A", tg[1][1], zeros)
+    for i in range(2):
+        sv = run("A", act.activation(bank(T.sv0, i), bank(T.Tg0, diff[i]), AF.Sign, bias=0.5))
+    run("A", act.activation(T.inj[:, :], T.zer[:, :], AF.Copy))
+    c0 = run("A", act.activation(T.rst[:, :], T.zer[:, :], AF.Copy))
+    run("A", act.activation(T.C0[:, 0:2 * NJ:2], T.zer[:, :], AF.Identity, bias=64.0))
+    run("A", act.activation(T.D[:, 8:NJ:9], T.zer[:, 0:M], AF.Copy))
+    for k in range(2):
+        run("A", act.activation(T.C1[:, k * NJ + 1:k * NJ + 2], T.zer[:, 0:1], AF.Identity, bias=B))
+        run("A", act.activation(T.C1[:, (k + 1) * NJ - 2:(k + 1) * NJ - 1], T.zer[:, 0:1], AF.Copy))
+    need("A", c0)
+    run("A", act.activation(T.inj[:, 8:NJ:9], T.zer[:, 0:M], AF.Identity, bias=16384.0))
+    consts = run("A", act.activation(T.rst[:, 0:NJ:9], T.zer[:, 0:M], AF.Identity, bias=B))
 
     def turned(ph, mine, mine_ready, land, way, minus):
         done = {}
@@ -157,14 +162,12 @@ def rank_program(g, core, T, topo):
             out = blk(T["bk%d" % (p // 2)], p % 2)
             if p == me:
                 need("P", mine_ready)
-                src = blk(mine, p)
-            else:
-                need("P", ("arr%d_%d" % (ph, p), dict(dests_of(p, h))[me]))
-                src = blk(land, p)
-            tok = run("P", ten.matmul(out, turn(way * me * p), src, True, minus is None))
             if minus is not None:
-                tok = run("P", ten.matmul(out, T.NI[:, :], minus(p), False, True))
-            done[p // 2] = tok
+                run("P", ten.matmul(out, T.NI[:, :], minus(p), True, False))
+            if p != me:
+                need("P", ("arr%d_%d" % (ph, p), dict(dests_of(p, h))[me]))
+            src = blk(mine if p == me else land, p)
+            done[p // 2] = run("P", ten.matmul(out, turn(way * me * p), src, minus is None, True))
         return done
 
     def check(r, mine_ready):
@@ -185,31 +188,60 @@ def rank_program(g, core, T, topo):
             ga = run("A", act.activation(T.D[:, e + 4:NJ:9], win.indirect(T.pl16[:, 8 * e + 32:8 * e + 40]), AF.Copy))
         need("V", gv, ga, consts)
         need("A", gv, ga, consts)
+
+        def part(buf, k):
+            return buf[:, k * NH:(k + 1) * NH]
+
         f = run("V", vec.tensor_tensor_scan(T.F[:, :], T.D[:, :], T.inj[:, :], 16384.0, OP.mult, OP.add))
-        ab = [run("A", act.activation(T.A[:, k * NH:(k + 1) * NH], T.D[:, k * NH:(k + 1) * NH], AF.Abs, bias=-0.5)) for k in range(2)]
-        for k in range(2):
+        ab, na, neg, suf, w = {}, {}, {}, {}, {}
+        for k in (1, 0):
+            ab[k] = run("A", act.activation(part(T.A, k), part(T.D, k), AF.Abs, bias=-0.5))
+
+        def before(k):
             need("V", ab[k])
-            lo, hi = (1, NH + 1) if k == 0 else (NH + 1, NJ)
+            lo, hi = k * NH + 1, (k + 1) * NH
             pre = run("V", vec.tensor_tensor_scan(T.C1[:, 2 * lo + 1:2 * hi:2], T.A[:, lo - 1:hi - 1], T.rst[:, lo:hi], B, OP.min, OP.max))
-            na = run("V", vec.tensor_scalar(T.NA[:, k * NH:(k + 1) * NH], T.A[:, k * NH:(k + 1) * NH], -1.0, None, OP.mult))
             need("A", pre)
-            lo = lo - 1 if k == 0 else lo
-            neg = run("A", act.activation(T.C0[:, 2 * lo + 1:2 * hi:2], T.C1[:, 2 * lo + 1:2 * hi:2], AF.Copy, scale=-1.0))
-        for i in range(2):
-            sc = run("A", act.activation(bank(T.sc, i), bank(T.dwin, same[i]), AF.Sign))
-        need("V", f, na)
-        run("V", vec.tensor_copy(T.A[:, 8:NJ:9], T.F[:, 7:NJ:9]))
-        nu = run("V", vec.memset(T.NA[:, 8:NJ:9], 64.0))
-        need("V", nu)
-        suf = run("V", vec.tensor_tensor_scan(T.C1[:, 2 * NJ - 4::-2], T.NA[:, NJ - 1:0:-1], T.A[:, NJ - 1:0:-1], 0.0, OP.max, OP.min))
+            neg[k] = run("A", act.activation(T.C0[:, 2 * lo - 1:2 * hi:2], T.C1[:, 2 * lo - 1:2 * hi:2], AF.Copy, scale=-1.0))
+
+        def negate(k):
+            na[k] = run("V", vec.tensor_scalar(part(T.NA, k), part(T.A, k), -1.0, None, OP.mult))
+
+        def start(k):
+            lo, hi = k * NH, (k + 1) * NH
+            need("V", f, na[k])
+            run("V", vec.tensor_copy(T.A[:, lo + 8:hi:9], T.F[:, lo + 7:hi:9]))
+            return run("V", vec.memset(T.NA[:, lo + 8:hi:9], 64.0))
+
+        def behind(k, ready):
+            need("V", ready)
+            top = (k + 1) * NH - 1
+            cols, to = slice(top, k * NH, -1), slice(2 * (top - 1), 2 * k * NH - 2 if k else None, -2)
+            suf[k] = run("V", vec.tensor_tensor_scan(T.C1[:, to], T.NA[:, cols], T.A[:, cols], 0.0, OP.max, OP.min))
+
+        def both(k):
+            need("V", suf[k], neg[k])
+            c = slice(2 * k * NH, 2 * (k + 1) * NH)
+            w[k] = run("V", vec.tensor_tensor_scan(T.C2[:, c], T.C0[:, c], T.C1[:, c], 0.0, OP.max, OP.min))
+
+        before(1)
+        negate(1)
+        before(0)
+        s1 = start(1)
+        negate(0)
+        behind(1, s1)
+        s2 = start(0)
         if r == 0:
             need("V", ("dr", 16))
             inv[0] = run("V", vec.tensor_copy(T.inv16[:, :], T.inv32[:, :]))
-        need("V", suf, neg)
-        w = run("V", vec.tensor_tensor_scan(T.C2[:, :], T.C0[:, :], T.C1[:, :], 0.0, OP.max, OP.min))
+        behind(0, s2)
+        both(1)
+        both(0)
+        for i in range(2):
+            sc = run("A", act.activation(bank(T.sc, i), bank(T.dwin, same[i]), AF.Sign))
         dst = T["Rs%d" % r]
-        need("V", w, sc, inv[0])
-        need("A", w, inv[0])
+        need("V", w[0], sc, inv[0])
+        need("A", w[0], inv[0])
         win = T.C2[:, 0:2 * NJ]
         a, b = [], []
         for i in range(2):
@@ -227,7 +259,7 @@ def rank_program(g, core, T, topo):
                 rf[0] = run("V", vec.tensor_tensor(bank(T.Rf, i), bank(dst, diff[i]), bank(T.so, i), OP.mult))
         return a[0]
 
-    def variables(r, rs, sv):
+    def variables(r, rs, sv, out):
         done = turned(2 * r + 1, T["Rs%d" % r], rs, T["Lr%d" % r], -1, None)
         rv, ev = T["Rv%d" % r], []
         need("V", sv)
@@ -244,14 +276,19 @@ def rank_program(g, core, T, topo):
         a = run("V", vec.tensor_copy(gd[:, 0:512], rv[:, 0:W].indirect(T.vl16[:, 0:32])))
         b = run("A", act.activation(gd[:, 512:1024], rv[:, 0:W].indirect(T.vl16[:, 32:64]), AF.Copy))
         need("P", x_in)
-        run("P", ten.matmul(T.tt[:, 0:256], eye, T.xs[:, :], True, False))
-        need("P", a)
-        for d in range(2):
-            run("P", ten.matmul(T.tt[:, 0:256], eye, gd[:, 256 * d:256 * d + 256], False, False))
-        need("P", b)
-        for d in range(2, 4):
-            t = run("P", ten.matmul(T.tt[:, 0:256], eye, gd[:, 256 * d:256 * d + 256], False, d == 3))
-        need("V", t)
+        t = {}
+        for k in range(2):
+            run("P", ten.matmul(T["tt%d" % k][:, 0:128], eye, T.xs[:, 128 * k:128 * k + 128], True, False))
+        for ready, ds in ((a, (0, 1)), (b, (2, 3))):
+            need("P", ready)
+            for k in range(2):
+                for d in ds:
+                    at = 256 * d + 128 * k
+                    t[k] = run("P", ten.matmul(T["tt%d" % k][:, 0:128], eye, gd[:, at:at + 128], False, d == 3))
+        need("V", t[0])
+        need("A", t[1])
+        return [run("V", vec.tensor_copy(out[:, 0:128], T.tt0[:, 0:128])),
+                run("A", act.activation(out[:, 128:256], T.tt1[:, 0:128], AF.Copy))]
 
     def own_r(p):
         b = p // 2
@@ -259,9 +296,8 @@ def rank_program(g, core, T, topo):
 
     inv, rf = [None], [None]
     rs = check(0, tg[0][0])
-    variables(0, rs, sv)
-    tw = run("V", vec.tensor_copy(T.Tw[:, :], T.tt[:, 0:256]))
-    tg = var_gather(1, T.Tw, [tw])
+    tw = variables(0, rs, sv, T.Tw)
+    tg = var_gather(1, T.Tw, tw)
     need("P", tg[1][1])
     for i in range(2):
         run("P", ten.matmul(bank(T["sg%d" % i], 0), eye, bank(T.Tg1, diff[i]), True, False))
@@ -269,9 +305,8 @@ def rank_program(g, core, T, topo):
         need("A", t)
         sv = run("A", act.activation(bank(T.sv1, i), bank(T["sg%d" % i], 0), AF.Sign, bias=0.5))
     rs = check(1, tg[0][0])
-    variables(1, rs, sv)
-    yt = run("V", vec.tensor_copy(T.ys[:, :], T.tt[:, 0:256]))
-    need("S", yt)
+    yt = variables(1, rs, sv, T.ys)
+    need("S", *yt)
     g.sync.dma_start(T.y[:, :], T.ys[:, :]).then_inc(T.sem.dy, 16)
     need("S", ("dy", 16))
     for q in ("V", "A", "P", "G"):

@@ -8,32 +8,37 @@ H = 2 * BK
 NJ = 9 * M
 NH = NJ // 2
 B = 51.0
+OFF = 64
+CUT = 96
 OP = AluOpType
 AF = ActivationFunctionType
+CALLS = [[(5, 4), (2, 4)], [(4, 2), (3, 2), (1, 2), (7, 2)], [(6, 8)]]
+ENG = {d: n for c in CALLS for d, n in c}
+AT_CHECKS = [0, 5, 2, 4, 1, 3, 7, 6]
+AT_VARS = [0, 5, 2, 3, 7, 4, 1, 6]
 
 SCRATCH = {
     "sn32": ("sbuf", [128, 80], "int32"), "pl32": ("sbuf", [128, 64], "int32"), "vl32": ("sbuf", [128, 64], "int32"),
     "sn16": ("sbuf", [128, 80], "uint16"), "pl16": ("sbuf", [128, 64], "uint16"), "vl16": ("sbuf", [128, 64], "uint16"),
     "ta": ("sbuf", [128, 64], "int32"), "tb": ("sbuf", [128, 64], "int32"), "tc": ("sbuf", [128, 64], "int32"),
     "td": ("sbuf", [128, 64], "int32"), "pc16": ("sbuf", [128, 64], "uint16"),
-    "num": ("sbuf", [128, 1024], "float32"), "invw": ("sbuf", [128, W], "float32"),
+    "num": ("sbuf", [128, 512], "float32"), "num2": ("sbuf", [128, 512], "float32"),
+    "iva": ("sbuf", [128, W], "float32"), "ivb": ("sbuf", [128, W], "float32"),
     "inv32": ("sbuf", [128, 80], "float32"), "inv16": ("sbuf", [128, 80], "uint16"),
-    "ei": ("sbuf", [128, 256], "float32"), "E": ("sbuf", [128, 256], "bfloat16"), "NI": ("sbuf", [128, 128], "bfloat16"),
+    "one": ("sbuf", [128, 256], "bfloat16"), "E": ("sbuf", [128, 256], "bfloat16"), "NI": ("sbuf", [128, 128], "bfloat16"),
     "xs": ("sbuf", [128, 256], "bfloat16"), "Tw": ("sbuf", [128, 256], "bfloat16"), "ys": ("sbuf", [128, 256], "float32"),
-    "dwin": ("sbuf", [128, W], "bfloat16"), "zer": ("sbuf", [128, NJ], "bfloat16"),
+    "dwin": ("sbuf", [128, W], "bfloat16"),
     "D": ("sbuf", [128, NJ], "bfloat16"), "A": ("sbuf", [128, NJ], "bfloat16"), "NA": ("sbuf", [128, NJ], "bfloat16"),
-    "F": ("sbuf", [128, NJ], "bfloat16"), "rst": ("sbuf", [128, NJ], "bfloat16"), "inj": ("sbuf", [128, NJ], "bfloat16"),
+    "F": ("sbuf", [128, NJ], "bfloat16"), "Z": ("sbuf", [128, NJ], "bfloat16"),
     "C0": ("sbuf", [128, 2 * NJ], "bfloat16"), "C1": ("sbuf", [128, 2 * NJ], "bfloat16"), "C2": ("sbuf", [128, 2 * NJ], "bfloat16"),
     "sc": ("sbuf", [128, H], "bfloat16"), "so": ("sbuf", [128, H], "bfloat16"), "Rf": ("sbuf", [128, H], "bfloat16"),
-    "bk0": ("psum", [128, 512], "float32"), "bk1": ("psum", [128, 512], "float32"),
-    "bk2": ("psum", [128, 512], "float32"), "bk3": ("psum", [128, 512], "float32"),
-    "tt0": ("psum", [128, 512], "float32"), "tt1": ("psum", [128, 512], "float32"),
-    "sg0": ("psum", [128, 512], "float32"), "sg1": ("psum", [128, 512], "float32"),
 }
+for _d in range(NR):
+    SCRATCH["bk%d" % _d] = ("psum", [128, 512], "float32")
 for _r in range(2):
     for _n, _w in (("Tg", W), ("Rs", W), ("Lm", W), ("Lr", W), ("Rv", W), ("Gv", 1024), ("sv", H)):
         SCRATCH["%s%d" % (_n, _r)] = ("sbuf", [128, _w], "bfloat16")
-SEMAPHORES = ["sV", "sA", "sP", "sG", "dx", "dsn", "dpl", "dvl", "dr", "dy", "ls"]
+SEMAPHORES = ["sV", "sA", "sP", "sG", "dx", "dsn", "dpl", "dvl", "df", "dr", "da", "dy", "ls"]
 SEMAPHORES += ["arr%d_%d" % (ph, p) for ph in range(4) for p in range(NR)]
 
 
@@ -57,7 +62,6 @@ def rank_program(g, core, T, topo):
         inst.then_inc(T.sem["s" + q], 1)
         return ("s" + q, cnt[q])
 
-    h = me // 4
     s0 = me // 2
     same = [s0, s0 ^ 2]
     diff = [s0 ^ 1, s0 ^ 3]
@@ -68,9 +72,19 @@ def rank_program(g, core, T, topo):
     def blk(buf, q):
         return buf[:, q * CAP:(q + 1) * CAP]
 
+    def half(buf, q):
+        b = q // 2
+        return blk(buf, 2 * (same.index(b) if b in same else diff.index(b)) + q % 2)
+
+    def ps(d):
+        return T["bk%d" % d][:, 0:CAP]
+
     def turn(k):
         s = (128 - 16 * (k % 8)) % 128
         return T.E[:, s:s + 128]
+
+    def const(ap, n, value):
+        return run("G", g.iota(ap, [[0, n]], value, 0, allow_small_or_imprecise_dtypes=True))
 
     eye = T.E[:, 0:128]
     g.sync.dma_start(T.sn32[:, :], T.sn[:, :]).then_inc(T.sem.dsn, 16)
@@ -78,23 +92,20 @@ def rank_program(g, core, T, topo):
     g.sync.dma_start(T.pl32[:, :], T.pl[:, :]).then_inc(T.sem.dpl, 16)
     act.dma_start(T.vl32[:, :], T.vl[:, :]).then_inc(T.sem.dvl, 16)
     sn_in, x_in, pl_in, vl_in = ("dsn", 16), ("dx", 16), ("dpl", 16), ("dvl", 16)
-    base = run("G", g.iota(T.num[:, 0:128], [[18, 128]], 1, 0, allow_small_or_imprecise_dtypes=True))
-    ei = run("G", g.iota(T.ei[:, :], [[0, 2], [1, 128]], 0, -1, allow_small_or_imprecise_dtypes=True))
-    need("A", base)
-    for e in range(1, 8):
-        num = run("A", act.activation(T.num[:, 128 * e:128 * e + 128], T.num[:, 0:128], AF.Identity, bias=2.0 * e))
-    fill = run("V", vec.memset(T.invw[:, :], 0.0))
-    zeros = run("V", vec.memset(T.zer[:, :], 0.0))
+    num = run("G", g.iota(T.num[:, :], [[2, 4], [18, 128]], 1 + OFF, 0, allow_small_or_imprecise_dtypes=True))
+    ones = run("V", vec.memset(T.one[:, :], 1.0))
+    need("A", ones)
+    run("A", act.activation(T.C1[:, 1:2 * NJ:NJ], T.one[:, 0:2], AF.Silu, bias=B - 1.0))
+    fill = run("V", vec.memset(T.iva[:, :], 0.0))
+    need("S", fill)
+    g.sync.dma_start(T.ivb[0:128:16, :], T.iva[0:128:16, :]).then_inc(T.sem.df, 16)
     need("V", sn_in)
     sn16 = run("V", vec.tensor_copy(T.sn16[:, :], T.sn32[:, :]))
 
-    def dests_of(p, k):
-        d = sorted([r for r in range(4 * k, 4 * k + 4) if r != p], key=lambda r: (r - p) % NR)
-        return list(zip(d, [2, 2, 4] if len(d) == 3 else [2, 2, 2, 2]))
-
     def send(ph, src, dst, k):
         tr, at = [], 0
-        for r, n in dests_of(me, k):
+        for d, n in CALLS[k]:
+            r = me ^ d
             c = T.cores[r]
             rid, pid, _s = topo.addr(c)
             eng = topo.engines(core, c)[at:at + n]
@@ -104,117 +115,137 @@ def rank_program(g, core, T, topo):
             cnt["ls"] += n
         g.remote_dma_fused(tr, local_sem=T.sem.ls)
 
+    def by_slots(ph, win, lst, dst, land, signs):
+        def v(d, lo=0, hi=CAP):
+            c = (me ^ d) * CAP
+            src = win.indirect(lst[:, (c + lo) // 16:(c + hi) // 16])
+            out = dst[:, c + lo:c + hi]
+            if signs is not None and not d & 2:
+                return run("V", vec.tensor_tensor(out, src, half(signs, me ^ d), OP.mult))
+            return run("V", vec.tensor_copy(out, src))
+
+        def a(d, lo=0, hi=CAP):
+            c = (me ^ d) * CAP
+            return run("A", act.activation(dst[:, c + lo:c + hi], win.indirect(lst[:, (c + lo) // 16:(c + hi) // 16]), AF.Copy))
+
+        t = [(v(5), a(2))]
+        v(4), a(3)
+        t.append((v(1), a(7)))
+        t.append((v(6, 0, CUT), a(6, CUT, CAP)))
+        own = v(0)
+        for k in range(3):
+            need("G", *t[k])
+            send(ph, dst, land, k)
+        return own, t[2][1]
+
     def var_gather(r, win, ready):
-        dst = T["Tg%d" % r]
         need("V", sn16, *ready)
         need("A", sn16, *ready)
-        a, b = [], []
-        for i in range(2):
-            s, d = same[i], diff[i]
-            a.append(run("V", vec.tensor_copy(bank(dst, s), win[:, 0:256].indirect(T.sn16[:, 20 * s:20 * s + 20]))))
-            b.append(run("A", act.activation(bank(dst, d), win[:, 0:256].indirect(T.sn16[:, 20 * d:20 * d + 20]), AF.Copy)))
-        for i in range(2):
-            need("G", a[i], b[i])
-            send(2 * r, dst, T["Lm%d" % r], h if i == 0 else 1 - h)
-        return a, b
+        return by_slots(2 * r, win[:, 0:256], T.sn16, T["Tg%d" % r], T["Lm%d" % r], None)
 
-    tg = var_gather(0, T.xs, [x_in])
+    own, tail = var_gather(0, T.xs, [x_in])
+    need("A", num)
+    num2 = run("A", act.activation(T.num2[:, :], T.num[:, :], AF.Silu, bias=8.0))
     need("V", pl_in)
     ta = run("V", vec.tensor_scalar(T.ta[:, :], T.pl32[:, :], 15, None, OP.bitwise_and))
     tb = run("V", vec.tensor_scalar(T.tb[:, :], T.pl32[:, :], 4, None, OP.arith_shift_right))
     need("V", ta)
     tc = run("V", vec.tensor_scalar(T.tc[:, :], T.ta[:, :], 80.0, None, OP.mult))
+    pl16 = run("V", vec.tensor_copy(T.pl16[:, :], T.pl32[:, :]))
     need("V", tb, tc)
     td = run("V", vec.tensor_tensor(T.td[:, :], T.tc[:, :], T.tb[:, :], OP.add))
-    need("V", ei)
-    eyes = run("V", vec.tensor_scalar(T.E[:, :], T.ei[:, :], 0.0, None, OP.is_equal))
-    need("V", td)
-    pc = run("V", vec.tensor_copy(T.pc16[:, :], T.td[:, :]))
-    pl16 = run("V", vec.tensor_copy(T.pl16[:, :], T.pl32[:, :]))
-    need("V", pc, fill, num)
-    scat = run("V", vec.tensor_copy(T.invw[:, 0:W].indirect(T.pc16[:, 0:64]), T.num[:, :]))
-    need("S", scat)
-    g.sync.dma_start(T.inv32[:, :], T.invw[0:128:16, :]).then_inc(T.sem.dr, 16)
-    need("V", eyes)
-    ni = run("V", vec.tensor_scalar(T.NI[:, :], eye, -1.0, None, OP.mult))
     need("V", vl_in)
     vl16 = run("V", vec.tensor_copy(T.vl16[:, :], T.vl32[:, :]))
-    need("A", tg[1][1], zeros)
-    for i in range(2):
-        sv = run("A", act.activation(bank(T.sv0, i), bank(T.Tg0, diff[i]), AF.Sign, bias=0.5))
-    run("A", act.activation(T.inj[:, :], T.zer[:, :], AF.Copy))
-    c0 = run("A", act.activation(T.rst[:, :], T.zer[:, :], AF.Copy))
-    run("A", act.activation(T.C0[:, 0:2 * NJ:2], T.zer[:, :], AF.Identity, bias=64.0))
-    run("A", act.activation(T.D[:, 8:NJ:9], T.zer[:, 0:M], AF.Copy))
-    for k in range(2):
-        run("A", act.activation(T.C1[:, k * NJ + 1:k * NJ + 2], T.zer[:, 0:1], AF.Identity, bias=B))
-        run("A", act.activation(T.C1[:, (k + 1) * NJ - 2:(k + 1) * NJ - 1], T.zer[:, 0:1], AF.Copy))
-    need("A", c0)
-    run("A", act.activation(T.inj[:, 8:NJ:9], T.zer[:, 0:M], AF.Identity, bias=16384.0))
-    consts = run("A", act.activation(T.rst[:, 0:NJ:9], T.zer[:, 0:M], AF.Identity, bias=B))
+    need("V", td)
+    pc = run("V", vec.tensor_copy(T.pc16[:, :], T.td[:, :]))
+    need("V", pc, fill, num, ("df", 16))
+    scat = run("V", vec.tensor_copy(T.iva[:, 0:W].indirect(T.pc16[:, 0:32]), T.num[:, :]))
+    need("A", pc, num2, ("df", 16))
+    scat2 = run("A", act.activation(T.ivb[:, 0:W].indirect(T.pc16[:, 32:64]), T.num2[:, :], AF.Silu))
+    need("S", scat)
+    g.sync.dma_start(T.inv32[:, :], T.iva[0:128:16, :]).then_inc(T.sem.dr, 16)
+    need("G", ones)
+    eyes = run("G", g.affine_select(T.E[:, :], T.one[:, :], [[0, 2], [-1, 128]], OP.is_equal, 0.0, 0, 1))
+    z = const(T.Z[:, :], NJ, 0)
+    const(T.D[:, 8:NJ:9], M, 0)
+    const(T.C1[:, NJ - 2:2 * NJ:NJ], 2, 0)
+    need("G", z)
+    z = const(T.Z[:, 8:NJ:9], M, int(B))
+    c0 = {1: const(T.C0[:, NJ:2 * NJ:2], NH, 64)}
+    need("G", scat2, ("dr", 16))
+    g.dma_start(T.inv32[:, :], T.ivb[0:128:16, :], accum_op=OP.add).then_inc(T.sem.da, 16)
+    c0[0] = const(T.C0[:, 0:NJ:2], NH, 64)
 
-    def turned(ph, mine, mine_ready, land, way, minus):
+    def turned(ph, order, mine, mine_ready, land, way, minus):
         done = {}
-        need("P", eyes, ni)
-        if minus is not None:
-            need("P", rf[0])
-        for p in [me, me ^ 1] + [2 * b + i for b in (diff[0], same[1], diff[1]) for i in range(2)]:
-            out = blk(T["bk%d" % (p // 2)], p % 2)
-            if p == me:
-                need("P", mine_ready)
-            if minus is not None:
-                run("P", ten.matmul(out, T.NI[:, :], minus(p), True, False))
-            if p != me:
-                need("P", ("arr%d_%d" % (ph, p), dict(dests_of(p, h))[me]))
-            src = blk(mine if p == me else land, p)
-            done[p // 2] = run("P", ten.matmul(out, turn(way * me * p), src, minus is None, True))
+        need("P", eyes)
+        for i, d in enumerate(order):
+            p = me ^ d
+            if minus and i == 3:
+                need("P", sv[0])
+                less_own((6, 7))
+            need("P", ("arr%d_%d" % (ph, p), ENG[d]) if d else mine_ready)
+            done[d] = run("P", ten.matmul(ps(d), turn(way * me * p), blk(land if d else mine, p), not minus, True))
         return done
 
+    def less_own(ds):
+        need("P", ni[0], rf[0])
+        for d in ds:
+            run("P", ten.matmul(ps(d), T.NI[:, :], own_r(me ^ d), True, False))
+
     def check(r, mine_ready):
-        done = turned(2 * r, T["Tg%d" % r], mine_ready, T["Lm%d" % r], 1, own_r if r else None)
+        done = turned(2 * r, AT_CHECKS, T["Tg%d" % r], mine_ready, T["Lm%d" % r], 1, r == 1)
         ev = []
-        for i in range(2):
-            b = same[i]
-            need("V", done[b])
-            ev.append(run("V", vec.tensor_scalar(bank(T.dwin, b), bank(T["bk%d" % b], 0), 0.5, None, OP.add)))
-            b = diff[i]
-            need("A", done[b])
-            ev.append(run("A", act.activation(bank(T.dwin, b), bank(T["bk%d" % b], 0), AF.Identity, bias=0.5)))
+        for d in AT_CHECKS:
+            out = blk(T.dwin, me ^ d)
+            if d in ((3, 7) if r == 0 else (2, 3, 7)):
+                need("A", done[d])
+                ev.append(run("A", act.activation(out, ps(d), AF.Identity, bias=1.0, scale=2.0)))
+            else:
+                need("V", done[d])
+                ev.append(run("V", vec.tensor_scalar(out, ps(d), 2.0, 1.0, OP.mult, OP.add)))
         win = T.dwin[:, 0:W]
         need("V", pl16, *ev)
         need("A", pl16, *ev)
         for e in range(4):
             gv = run("V", vec.tensor_copy(T.D[:, e:NJ:9], win.indirect(T.pl16[:, 8 * e:8 * e + 8])))
             ga = run("A", act.activation(T.D[:, e + 4:NJ:9], win.indirect(T.pl16[:, 8 * e + 32:8 * e + 40]), AF.Copy))
-        need("V", gv, ga, consts)
-        need("A", gv, ga, consts)
+        need("V", gv, ga, z)
+        need("A", gv, ga, z)
 
         def part(buf, k):
             return buf[:, k * NH:(k + 1) * NH]
 
-        f = run("V", vec.tensor_tensor_scan(T.F[:, :], T.D[:, :], T.inj[:, :], 16384.0, OP.mult, OP.add))
-        ab, na, neg, suf, w = {}, {}, {}, {}, {}
+        f = run("V", vec.tensor_tensor_scan(T.F[:, :], T.D[:, :], T.Z[:, :], B, OP.mult, OP.add))
+        ab, na, lim, neg, suf, w, fs = {}, {}, {}, {}, {}, {}, {}
         for k in (1, 0):
-            ab[k] = run("A", act.activation(part(T.A, k), part(T.D, k), AF.Abs, bias=-0.5))
+            ab[k] = run("A", act.activation(part(T.A, k), part(T.D, k), AF.Abs, bias=-0.5, scale=0.5))
 
         def before(k):
             need("V", ab[k])
             lo, hi = k * NH + 1, (k + 1) * NH
-            pre = run("V", vec.tensor_tensor_scan(T.C1[:, 2 * lo + 1:2 * hi:2], T.A[:, lo - 1:hi - 1], T.rst[:, lo:hi], B, OP.min, OP.max))
-            need("A", pre)
+            pre = run("V", vec.tensor_tensor_scan(T.C1[:, 2 * lo + 1:2 * hi:2], T.A[:, lo - 1:hi - 1], T.Z[:, lo - 1:hi - 1], B, OP.min, OP.max))
+            need("A", pre, c0[k])
             neg[k] = run("A", act.activation(T.C0[:, 2 * lo - 1:2 * hi:2], T.C1[:, 2 * lo - 1:2 * hi:2], AF.Copy, scale=-1.0))
 
         def negate(k):
-            na[k] = run("V", vec.tensor_scalar(part(T.NA, k), part(T.A, k), -1.0, None, OP.mult))
+            if k:
+                na[k] = run("V", vec.tensor_scalar(part(T.NA, k), part(T.A, k), -1.0, None, OP.mult))
+            else:
+                need("A", ab[k])
+                na[k] = run("A", act.activation(part(T.NA, k), part(T.A, k), AF.Copy, scale=-1.0))
+
+        def limit(k):
+            need("G", na[k])
+            lim[k] = const(T.NA[:, k * NH + 8:(k + 1) * NH:9], M // 2, 64)
 
         def start(k):
             lo, hi = k * NH, (k + 1) * NH
             need("V", f, na[k])
-            run("V", vec.tensor_copy(T.A[:, lo + 8:hi:9], T.F[:, lo + 7:hi:9]))
-            return run("V", vec.memset(T.NA[:, lo + 8:hi:9], 64.0))
+            fs[k] = run("V", vec.tensor_copy(T.A[:, lo + 8:hi:9], T.F[:, lo + 7:hi:9]))
 
-        def behind(k, ready):
-            need("V", ready)
+        def behind(k):
+            need("V", fs[k], lim[k])
             top = (k + 1) * NH - 1
             cols, to = slice(top, k * NH, -1), slice(2 * (top - 1), 2 * k * NH - 2 if k else None, -2)
             suf[k] = run("V", vec.tensor_tensor_scan(T.C1[:, to], T.NA[:, cols], T.A[:, cols], 0.0, OP.max, OP.min))
@@ -224,88 +255,89 @@ def rank_program(g, core, T, topo):
             c = slice(2 * k * NH, 2 * (k + 1) * NH)
             w[k] = run("V", vec.tensor_tensor_scan(T.C2[:, c], T.C0[:, c], T.C1[:, c], 0.0, OP.max, OP.min))
 
+        negate(0)
         before(1)
         negate(1)
         before(0)
-        s1 = start(1)
-        negate(0)
-        behind(1, s1)
-        s2 = start(0)
-        if r == 0:
-            need("V", ("dr", 16))
-            inv[0] = run("V", vec.tensor_copy(T.inv16[:, :], T.inv32[:, :]))
-        behind(0, s2)
+        limit(1)
+        limit(0)
+        start(1)
+        behind(1)
+        start(0)
+        behind(0)
         both(1)
+        if r == 0:
+            need("V", ("da", 16))
+            inv[0] = run("V", vec.tensor_scalar(T.inv16[:, :], T.inv32[:, :], 0.25 - OFF, 0.0, OP.add, OP.max))
         both(0)
         for i in range(2):
             sc = run("A", act.activation(bank(T.sc, i), bank(T.dwin, same[i]), AF.Sign))
         dst = T["Rs%d" % r]
         need("V", w[0], sc, inv[0])
         need("A", w[0], inv[0])
-        win = T.C2[:, 0:2 * NJ]
-        a, b = [], []
-        for i in range(2):
-            s, d = same[i], diff[i]
-            a.append(run("V", vec.tensor_tensor(bank(dst, s), win.indirect(T.inv16[:, 20 * s:20 * s + 20]), bank(T.sc, i), OP.mult)))
-            b.append(run("A", act.activation(bank(dst, d), win.indirect(T.inv16[:, 20 * d:20 * d + 20]), AF.Copy)))
-        for i in range(2):
-            need("G", a[i], b[i])
-            send(2 * r + 1, dst, T["Lr%d" % r], h if i == 0 else 1 - h)
+        rs, tail = by_slots(2 * r + 1, T.C2[:, 0:2 * NJ], T.inv16, dst, T["Lr%d" % r], T.sc)
         if r == 0:
             for i in range(2):
                 so = run("A", act.activation(bank(T.so, i), bank(T.dwin, diff[i]), AF.Sign))
-            need("V", so, b[1])
+            for i in range(2):
+                sv[0] = run("A", act.activation(bank(T.sv0, i), bank(T.Tg0, diff[i]), AF.Sign, bias=0.5))
+            need("A", eyes)
+            ni[0] = run("A", act.activation(T.NI[:, :], eye, AF.Copy, scale=-1.0))
+            need("V", rs, so)
             for i in range(2):
                 rf[0] = run("V", vec.tensor_tensor(bank(T.Rf, i), bank(dst, diff[i]), bank(T.so, i), OP.mult))
-        return a[0]
+        return rs
 
-    def variables(r, rs, sv, out):
-        done = turned(2 * r + 1, T["Rs%d" % r], rs, T["Lr%d" % r], -1, None)
-        rv, ev = T["Rv%d" % r], []
-        need("V", sv)
-        for i in range(2):
-            b = same[i]
-            need("A", done[b])
-            ev.append(run("A", act.activation(bank(rv, b), bank(T["bk%d" % b], 0), AF.Copy)))
-            b = diff[i]
-            need("V", done[b])
-            ev.append(run("V", vec.tensor_tensor(bank(rv, b), bank(T["bk%d" % b], 0), bank(T["sv%d" % r], i), OP.mult)))
+    def variables(r, rs, out):
+        done = turned(2 * r + 1, AT_VARS, T["Rs%d" % r], rs, T["Lr%d" % r], -1, False)
+        rv, ev = T["Rv%d" % r], {}
+        need("V", sv[0])
+        for d in AT_VARS:
+            if d & 2:
+                need("V", done[d])
+                ev[d] = run("V", vec.tensor_tensor(blk(rv, me ^ d), ps(d), half(T["sv%d" % r], me ^ d), OP.mult))
+            else:
+                need("A", done[d])
+                ev[d] = run("A", act.activation(blk(rv, me ^ d), ps(d), AF.Copy))
         gd = T["Gv%d" % r]
-        need("V", vl16, *ev)
-        need("A", vl16, *ev)
-        a = run("V", vec.tensor_copy(gd[:, 0:512], rv[:, 0:W].indirect(T.vl16[:, 0:32])))
-        b = run("A", act.activation(gd[:, 512:1024], rv[:, 0:W].indirect(T.vl16[:, 32:64]), AF.Copy))
-        need("P", x_in)
-        t = {}
-        for k in range(2):
-            run("P", ten.matmul(T["tt%d" % k][:, 0:128], eye, T.xs[:, 128 * k:128 * k + 128], True, False))
-        for ready, ds in ((a, (0, 1)), (b, (2, 3))):
-            need("P", ready)
-            for k in range(2):
-                for d in ds:
-                    at = 256 * d + 128 * k
-                    t[k] = run("P", ten.matmul(T["tt%d" % k][:, 0:128], eye, gd[:, at:at + 128], False, d == 3))
-        need("V", t[0])
-        need("A", t[1])
-        return [run("V", vec.tensor_copy(out[:, 0:128], T.tt0[:, 0:128])),
-                run("A", act.activation(out[:, 128:256], T.tt1[:, 0:128], AF.Copy))]
+        need("V", vl16, *ev.values())
+        need("A", vl16, *ev.values())
+
+        def quarter(d):
+            return gd[:, 256 * d:256 * d + 256], rv[:, 0:W].indirect(T.vl16[:, 16 * d:16 * d + 16])
+
+        got = {}
+        for d in range(2):
+            got[d] = run("V", vec.tensor_copy(*quarter(d)))
+            got[d + 2] = run("A", act.activation(*quarter(d + 2), AF.Copy))
+        tt = T.bk0[:, 0:256]
+        need("P", x_in, ev[0])
+        run("P", ten.matmul(tt, eye, T.xs[:, :], True, False))
+        for d in (0, 2, 3):
+            need("P", got[d])
+            t = run("P", ten.matmul(tt, eye, gd[:, 256 * d:256 * d + 256], False, d == 3))
+        need("V", got[1], t)
+        return [run("V", vec.tensor_tensor(out[:, :], tt, gd[:, 256:512], OP.add))]
 
     def own_r(p):
-        b = p // 2
-        return blk(T.Rs0, p) if b in same else blk(T.Rf, 2 * diff.index(b) + p % 2)
+        return blk(T.Rs0, p) if p // 2 in same else half(T.Rf, p)
 
-    inv, rf = [None], [None]
-    rs = check(0, tg[0][0])
-    tw = variables(0, rs, sv, T.Tw)
-    tg = var_gather(1, T.Tw, tw)
-    need("P", tg[1][1])
+    inv, rf, sv, ni = [None], [None], [None], [None]
+    rs = check(0, own)
+    tw = variables(0, rs, T.Tw)
+    need("P", ni[0], *tw)
+    sg = [bank(T["bk%d" % (6 + i)], 0) for i in range(2)]
     for i in range(2):
-        run("P", ten.matmul(bank(T["sg%d" % i], 0), eye, bank(T.Tg1, diff[i]), True, False))
-        t = run("P", ten.matmul(bank(T["sg%d" % i], 0), T.NI[:, :], bank(T.Rv0, diff[i]), False, True))
+        run("P", ten.matmul(sg[i], T.NI[:, :], bank(T.Rv0, diff[i]), True, False))
+    less_own(range(6))
+    own, tail = var_gather(1, T.Tw, tw)
+    need("P", own, tail)
+    for i in range(2):
+        t = run("P", ten.matmul(sg[i], eye, bank(T.Tg1, diff[i]), False, True))
         need("A", t)
-        sv = run("A", act.activation(bank(T.sv1, i), bank(T["sg%d" % i], 0), AF.Sign, bias=0.5))
-    rs = check(1, tg[0][0])
-    yt = variables(1, rs, sv, T.ys)
+        sv[0] = run("A", act.activation(bank(T.sv1, i), sg[i], AF.Sign, bias=0.5))
+    rs = check(1, own)
+    yt = variables(1, rs, T.ys)
     need("S", *yt)
     g.sync.dma_start(T.y[:, :], T.ys[:, :]).then_inc(T.sem.dy, 16)
     need("S", ("dy", 16))

@@ -9,17 +9,19 @@ NJ = 9 * M
 NH = NJ // 2
 B = 51.0
 OFF = 64
-CUT = 96
 OP = AluOpType
 AF = ActivationFunctionType
-CALLS = [[(5, 4), (2, 4)], [(4, 2), (3, 2), (1, 2), (7, 2)], [(6, 8)]]
-ENG = {d: n for c in CALLS for d, n in c}
-AT_CHECKS = [0, 5, 2, 4, 1, 3, 7, 6]
-AT_VARS = [0, 5, 2, 3, 7, 4, 1, 6]
+RAW = 5
+TO_CHECKS = {"V": "g7 g4 g1 g0", "A": "g3 g2 g6 c4 c1", "recv": "V0 A5 V7 A3 V2 A6",
+             "calls": [[(5, 0, 8)], [(7, 0, 4), (3, 4, 4)], [(6, 0, 4), (2, 4, 4)], [(4, 0, 4), (1, 4, 4)]]}
+TO_VARS = {"V": "g7 g5 g4 g1 g0", "A": "g3 g2 g6 c5 c4 c1", "recv": "A0 V3 V7 V2 V6",
+           "calls": [[(3, 0, 8)], [(7, 0, 4), (2, 4, 4)], [(6, 0, 4), (5, 4, 4)], [(4, 0, 4), (1, 4, 4)]]}
+PLAN = {0: dict(TO_CHECKS, recv="V0 A7 A3 V5 V2 A6"), 1: TO_VARS, 2: TO_CHECKS, 3: TO_VARS}
 
 SCRATCH = {
     "sn32": ("sbuf", [128, 80], "int32"), "pl32": ("sbuf", [128, 64], "int32"), "vl32": ("sbuf", [128, 64], "int32"),
     "sn16": ("sbuf", [128, 80], "uint16"), "pl16": ("sbuf", [128, 64], "uint16"), "vl16": ("sbuf", [128, 64], "uint16"),
+    "rn32": ("sbuf", [128, 10], "int32"), "rn16": ("sbuf", [128, 10], "uint16"),
     "ta": ("sbuf", [128, 64], "int32"), "tb": ("sbuf", [128, 64], "int32"), "tc": ("sbuf", [128, 64], "int32"),
     "td": ("sbuf", [128, 64], "int32"), "pc16": ("sbuf", [128, 64], "uint16"),
     "num": ("sbuf", [128, 512], "float32"), "num2": ("sbuf", [128, 512], "float32"),
@@ -27,18 +29,18 @@ SCRATCH = {
     "inv32": ("sbuf", [128, 80], "float32"), "inv16": ("sbuf", [128, 80], "uint16"),
     "one": ("sbuf", [128, 256], "bfloat16"), "E": ("sbuf", [128, 256], "bfloat16"), "NI": ("sbuf", [128, 128], "bfloat16"),
     "xs": ("sbuf", [128, 256], "bfloat16"), "Tw": ("sbuf", [128, 256], "bfloat16"), "ys": ("sbuf", [128, 256], "float32"),
-    "dwin": ("sbuf", [128, W], "bfloat16"),
     "D": ("sbuf", [128, NJ], "bfloat16"), "A": ("sbuf", [128, NJ], "bfloat16"), "NA": ("sbuf", [128, NJ], "bfloat16"),
-    "F": ("sbuf", [128, NJ], "bfloat16"), "Z": ("sbuf", [128, NJ], "bfloat16"),
+    "F": ("sbuf", [128, NJ], "bfloat16"), "Z": ("sbuf", [128, NH], "bfloat16"),
     "C0": ("sbuf", [128, 2 * NJ], "bfloat16"), "C1": ("sbuf", [128, 2 * NJ], "bfloat16"), "C2": ("sbuf", [128, 2 * NJ], "bfloat16"),
     "sc": ("sbuf", [128, H], "bfloat16"), "so": ("sbuf", [128, H], "bfloat16"), "Rf": ("sbuf", [128, H], "bfloat16"),
 }
 for _d in range(NR):
     SCRATCH["bk%d" % _d] = ("psum", [128, 512], "float32")
 for _r in range(2):
-    for _n, _w in (("Tg", W), ("Rs", W), ("Lm", W), ("Lr", W), ("Rv", W), ("Gv", 1024), ("sv", H)):
+    for _n, _w in (("Tg", W), ("Rs", W), ("Lm", W), ("Lr", W), ("Xm", W), ("Xr", W), ("Dw", W), ("Rv", W), ("Gv", 1024), ("sv", H),
+                   ("rx", 256)):
         SCRATCH["%s%d" % (_n, _r)] = ("sbuf", [128, _w], "bfloat16")
-SEMAPHORES = ["sV", "sA", "sP", "sG", "dx", "dsn", "dpl", "dvl", "df", "dr", "da", "dy", "ls"]
+SEMAPHORES = ["sV", "sA", "sP", "sG", "dx", "dsn", "dpl", "dvl", "df", "dr", "da", "dy", "ls", "rn"]
 SEMAPHORES += ["arr%d_%d" % (ph, p) for ph in range(4) for p in range(NR)]
 
 
@@ -79,7 +81,8 @@ def rank_program(g, core, T, topo):
     def ps(d):
         return T["bk%d" % d][:, 0:CAP]
 
-    def turn(k):
+    def turn(ph, r):
+        k = me * r if ph % 2 == 0 else -me * r
         s = (128 - 16 * (k % 8)) % 128
         return T.E[:, s:s + 128]
 
@@ -94,56 +97,118 @@ def rank_program(g, core, T, topo):
     sn_in, x_in, pl_in, vl_in = ("dsn", 16), ("dx", 16), ("dpl", 16), ("dvl", 16)
     num = run("G", g.iota(T.num[:, :], [[2, 4], [18, 128]], 1 + OFF, 0, allow_small_or_imprecise_dtypes=True))
     ones = run("V", vec.memset(T.one[:, :], 1.0))
+    need("G", ones)
+    eyes = run("G", g.affine_select(T.E[:, :], T.one[:, :], [[0, 2], [-1, 128]], OP.is_equal, 0.0, 0, 1))
     need("A", ones)
     run("A", act.activation(T.C1[:, 1:2 * NJ:NJ], T.one[:, 0:2], AF.Silu, bias=B - 1.0))
+    zero = run("V", vec.memset(T.Z[:, :], 0.0))
     fill = run("V", vec.memset(T.iva[:, :], 0.0))
     need("S", fill)
     g.sync.dma_start(T.ivb[0:128:16, :], T.iva[0:128:16, :]).then_inc(T.sem.df, 16)
     need("V", sn_in)
     sn16 = run("V", vec.tensor_copy(T.sn16[:, :], T.sn32[:, :]))
 
-    def send(ph, src, dst, k):
-        tr, at = [], 0
-        for d, n in CALLS[k]:
-            r = me ^ d
-            c = T.cores[r]
-            rid, pid, _s = topo.addr(c)
-            eng = topo.engines(core, c)[at:at + n]
-            at += n
-            tr.append(RemoteDMATransfer(dst_ids=[DstId(rid=rid, pnc=pid)], dma_engine_mask=sum(1 << e for e in eng),
-                                        remote_sem=T.sem["arr%d_%d" % (ph, me)], src=blk(src, r), dst=blk(dst, me)))
+    def toks(ph, name, kind=None):
+        return [(t[0], int(t[1:])) for t in PLAN[ph][name].split() if kind is None or t[0] == kind]
+
+    def turned_here(ph):
+        return [d for q in "VA" for k, d in toks(ph, q, "c")]
+
+    def arrived(ph, d):
+        return ("arr%d_%d" % (ph, me ^ d), [n for c in PLAN[ph]["calls"] for e, o, n in c if e == d][0])
+
+    def send(items):
+        tr = []
+        for d, o, n, src, dst, sem in items:
+            to = T.cores[me ^ d]
+            rid, pid, _s = topo.addr(to)
+            tr.append(RemoteDMATransfer(dst_ids=[DstId(rid=rid, pnc=pid)], dma_engine_mask=sum(1 << e for e in topo.engines(core, to)[o:o + n]),
+                                        remote_sem=T.sem[sem], src=src, dst=dst))
             cnt["ls"] += n
         g.remote_dma_fused(tr, local_sem=T.sem.ls)
 
-    def by_slots(ph, win, lst, dst, land, signs):
-        def v(d, lo=0, hi=CAP):
-            c = (me ^ d) * CAP
-            src = win.indirect(lst[:, (c + lo) // 16:(c + hi) // 16])
-            out = dst[:, c + lo:c + hi]
-            if signs is not None and not d & 2:
-                return run("V", vec.tensor_tensor(out, src, half(signs, me ^ d), OP.mult))
+    def send_raw(ph, win):
+        d, o, n = PLAN[ph]["calls"][0][0]
+        send([(d, o, n, win[:, :], T["rx%d" % (ph // 2)][:, :], "arr%d_%d" % (ph, me))])
+
+    def drain(ph, q, out, src):
+        if ph % 2 == 0:
+            if q == "V":
+                return run("V", vec.tensor_scalar(out, src, 2.0, 1.0, OP.mult, OP.add))
+            return run("A", act.activation(out, src, AF.Identity, bias=1.0, scale=2.0))
+        if q == "V":
             return run("V", vec.tensor_copy(out, src))
+        return run("A", act.activation(out, src, AF.Copy))
 
-        def a(d, lo=0, hi=CAP):
-            c = (me ^ d) * CAP
-            return run("A", act.activation(dst[:, c + lo:c + hi], win.indirect(lst[:, (c + lo) // 16:(c + hi) // 16]), AF.Copy))
+    def by_slots(ph, win, lst, bufs, ready):
+        src, land, xsrc, xland = bufs
+        xs, got, out, trn = turned_here(ph), {}, {}, {}
+        need("V", *ready)
+        need("A", *ready)
 
-        t = [(v(5), a(2))]
-        v(4), a(3)
-        t.append((v(1), a(7)))
-        t.append((v(6, 0, CUT), a(6, CUT, CAP)))
-        own = v(0)
-        for k in range(3):
-            need("G", *t[k])
-            send(ph, dst, land, k)
-        return own, t[2][1]
+        def gather(q, d):
+            r = me ^ d
+            i, o = win.indirect(lst[:, r * CAP // 16:(r + 1) * CAP // 16]), blk(src, r)
+            if q == "A":
+                return run("A", act.activation(o, i, AF.Copy))
+            if ph == 2 and not d & 2:
+                return run("V", vec.tensor_tensor(o, i, blk(T.Rv0, r), OP.subtract))
+            if ph % 2 and not d & 2:
+                return run("V", vec.tensor_tensor(o, i, half(T.sc, r), OP.mult))
+            return run("V", vec.tensor_copy(o, i))
 
-    def var_gather(r, win, ready):
-        need("V", sn16, *ready)
-        need("A", sn16, *ready)
-        return by_slots(2 * r, win[:, 0:256], T.sn16, T["Tg%d" % r], T["Lm%d" % r], None)
+        todo = {q: toks(ph, q) for q in "VA"}
+        while todo["V"] or todo["A"]:
+            for q in "VA":
+                while todo[q] and (todo[q][0][0] == "g" or todo[q][0][1] in trn):
+                    kind, d = todo[q].pop(0)
+                    r = me ^ d
+                    if kind == "c":
+                        need(q, trn[d])
+                        out[d] = drain(ph, q, blk(xsrc, r), ps(d))
+                        continue
+                    got[d] = gather(q, d)
+                    if d in xs:
+                        need("P", eyes, got[d])
+                        trn[d] = run("P", ten.matmul(ps(d), turn(ph, r), blk(src, r), True, True))
+        for c in PLAN[ph]["calls"][(ph + 1) % 2:]:
+            for d, o, n in c:
+                need("G", out[d] if d in xs else got[d])
+            send([(d, o, n, blk(xsrc if d in xs else src, me ^ d), blk(xland if d in xs else land, me), "arr%d_%d" % (ph, me))
+                  for d, o, n in c])
+        return got
 
-    own, tail = var_gather(0, T.xs, [x_in])
+    def taken(ph, mine, mine_ready, land, rv, early=None):
+        done, ev, left = {}, {}, [early] if early else []
+        for q, d in toks(ph, "recv"):
+            p = me ^ d
+            need("P", rawg[ph] if (ph, d) in ((0, RAW), (2, RAW)) else arrived(ph, d) if d else mine_ready)
+            done[d] = run("P", ten.matmul(ps(d), turn(ph, p), blk(land if d else mine, p), not (ph == 2 and (d & 2 or d == RAW)), True))
+            if left:
+                left.pop()()
+        for q, d in toks(ph, "recv"):
+            p = me ^ d
+            need(q, done[d])
+            if ph % 2 and d & 2:
+                need("V", sv[0])
+                ev[d] = run("V", vec.tensor_tensor(blk(rv, p), ps(d), half(T["sv%d" % (ph // 2)], p), OP.mult))
+            else:
+                ev[d] = drain(ph, q, blk(rv, p), ps(d))
+        for d in turned_here(ph):
+            ev[d] = arrived(ph, d)
+        return ev
+
+    def gather_raw(ph):
+        need("V", arrived(ph, RAW))
+        win = T["rx%d" % (ph // 2)][:, 0:256]
+        rawg[ph] = run("V", vec.tensor_copy(blk(T["Lm%d" % (ph // 2)], me ^ RAW), win.indirect(T.rn16[:, :])))
+
+    inv, rf, sv, ni, rawg = [None], [None], [None], [None], {}
+    need("G", x_in)
+    send_raw(0, T.xs)
+    need("G", sn_in)
+    send([(RAW, 0, 8, T.sn32[:, (me ^ RAW) * 10:(me ^ RAW) * 10 + 10], T.rn32[:, :], "rn")])
+    own = by_slots(0, T.xs[:, 0:256], T.sn16, (T.Tg0, T.Lm0, T.Xm0, T.Dw0), [sn16, x_in])[0]
     need("A", num)
     num2 = run("A", act.activation(T.num2[:, :], T.num[:, :], AF.Silu, bias=8.0))
     need("V", pl_in)
@@ -164,49 +229,34 @@ def rank_program(g, core, T, topo):
     scat2 = run("A", act.activation(T.ivb[:, 0:W].indirect(T.pc16[:, 32:64]), T.num2[:, :], AF.Silu))
     need("S", scat)
     g.sync.dma_start(T.inv32[:, :], T.iva[0:128:16, :]).then_inc(T.sem.dr, 16)
-    need("G", ones)
-    eyes = run("G", g.affine_select(T.E[:, :], T.one[:, :], [[0, 2], [-1, 128]], OP.is_equal, 0.0, 0, 1))
-    z = const(T.Z[:, :], NJ, 0)
+    need("V", ("rn", 8))
+    rn16 = run("V", vec.tensor_copy(T.rn16[:, :], T.rn32[:, :]))
+    need("V", rn16)
+    gather_raw(0)
+    need("G", zero)
+    const(T.Z[:, 8:NH:9], M // 2, int(B))
     const(T.D[:, 8:NJ:9], M, 0)
-    const(T.C1[:, NJ - 2:2 * NJ:NJ], 2, 0)
-    need("G", z)
-    z = const(T.Z[:, 8:NJ:9], M, int(B))
-    c0 = {1: const(T.C0[:, NJ:2 * NJ:2], NH, 64)}
+    z = const(T.C1[:, NJ - 2:2 * NJ:NJ], 2, 0)
+    c0 = {k: const(T.C0[:, k * NJ:(k + 1) * NJ:2], NH, 64) for k in (1, 0)}
     need("G", scat2, ("dr", 16))
     g.dma_start(T.inv32[:, :], T.ivb[0:128:16, :], accum_op=OP.add).then_inc(T.sem.da, 16)
-    c0[0] = const(T.C0[:, 0:NJ:2], NH, 64)
-
-    def turned(ph, order, mine, mine_ready, land, way, minus):
-        done = {}
-        need("P", eyes)
-        for i, d in enumerate(order):
-            p = me ^ d
-            if minus and i == 3:
-                need("P", sv[0])
-                less_own((6, 7))
-            need("P", ("arr%d_%d" % (ph, p), ENG[d]) if d else mine_ready)
-            done[d] = run("P", ten.matmul(ps(d), turn(way * me * p), blk(land if d else mine, p), not minus, True))
-        return done
 
     def less_own(ds):
         need("P", ni[0], rf[0])
         for d in ds:
-            run("P", ten.matmul(ps(d), T.NI[:, :], own_r(me ^ d), True, False))
+            run("P", ten.matmul(ps(d), T.NI[:, :], half(T.Rf, me ^ d) if d & 2 else blk(T.Rs0, me ^ d), True, False))
 
     def check(r, mine_ready):
-        done = turned(2 * r, AT_CHECKS, T["Tg%d" % r], mine_ready, T["Lm%d" % r], 1, r == 1)
-        ev = []
-        for d in AT_CHECKS:
-            out = blk(T.dwin, me ^ d)
-            if d in ((3, 7) if r == 0 else (2, 3, 7)):
-                need("A", done[d])
-                ev.append(run("A", act.activation(out, ps(d), AF.Identity, bias=1.0, scale=2.0)))
-            else:
-                need("V", done[d])
-                ev.append(run("V", vec.tensor_scalar(out, ps(d), 2.0, 1.0, OP.mult, OP.add)))
-        win = T.dwin[:, 0:W]
-        need("V", pl16, *ev)
-        need("A", pl16, *ev)
+        dwin = T["Dw%d" % r]
+
+        def late():
+            need("P", sv[0])
+            less_own((6, 7))
+
+        ev = taken(2 * r, T["Tg%d" % r], mine_ready, T["Lm%d" % r], dwin, late if r else None)
+        win = dwin[:, 0:W]
+        need("V", pl16, *ev.values())
+        need("A", pl16, *ev.values())
         for e in range(4):
             gv = run("V", vec.tensor_copy(T.D[:, e:NJ:9], win.indirect(T.pl16[:, 8 * e:8 * e + 8])))
             ga = run("A", act.activation(T.D[:, e + 4:NJ:9], win.indirect(T.pl16[:, 8 * e + 32:8 * e + 40]), AF.Copy))
@@ -216,20 +266,24 @@ def rank_program(g, core, T, topo):
         def part(buf, k):
             return buf[:, k * NH:(k + 1) * NH]
 
-        f = run("V", vec.tensor_tensor_scan(T.F[:, :], T.D[:, :], T.Z[:, :], B, OP.mult, OP.add))
-        ab, na, lim, neg, suf, w, fs = {}, {}, {}, {}, {}, {}, {}
+        ab, na, lim, neg, suf, w, fs, f, pre = {}, {}, {}, {}, {}, {}, {}, {}, {}
         for k in (1, 0):
+            f[k] = run("V", vec.tensor_tensor_scan(part(T.F, k), part(T.D, k), T.Z[:, :], B, OP.mult, OP.add))
             ab[k] = run("A", act.activation(part(T.A, k), part(T.D, k), AF.Abs, bias=-0.5, scale=0.5))
 
         def before(k):
             need("V", ab[k])
             lo, hi = k * NH + 1, (k + 1) * NH
-            pre = run("V", vec.tensor_tensor_scan(T.C1[:, 2 * lo + 1:2 * hi:2], T.A[:, lo - 1:hi - 1], T.Z[:, lo - 1:hi - 1], B, OP.min, OP.max))
-            need("A", pre, c0[k])
+            pre[k] = run("V", vec.tensor_tensor_scan(T.C1[:, 2 * lo + 1:2 * hi:2], T.A[:, lo - 1:hi - 1], T.Z[:, :NH - 1], B, OP.min, OP.max))
+
+        def negative(k):
+            lo, hi = k * NH + 1, (k + 1) * NH
+            need("A", pre[k], c0[k])
             neg[k] = run("A", act.activation(T.C0[:, 2 * lo - 1:2 * hi:2], T.C1[:, 2 * lo - 1:2 * hi:2], AF.Copy, scale=-1.0))
 
         def negate(k):
             if k:
+                need("V", ab[k])
                 na[k] = run("V", vec.tensor_scalar(part(T.NA, k), part(T.A, k), -1.0, None, OP.mult))
             else:
                 need("A", ab[k])
@@ -241,7 +295,7 @@ def rank_program(g, core, T, topo):
 
         def start(k):
             lo, hi = k * NH, (k + 1) * NH
-            need("V", f, na[k])
+            need("V", f[k], na[k], pre[k])
             fs[k] = run("V", vec.tensor_copy(T.A[:, lo + 8:hi:9], T.F[:, lo + 7:hi:9]))
 
         def behind(k):
@@ -256,11 +310,13 @@ def rank_program(g, core, T, topo):
             w[k] = run("V", vec.tensor_tensor_scan(T.C2[:, c], T.C0[:, c], T.C1[:, c], 0.0, OP.max, OP.min))
 
         negate(0)
-        before(1)
         negate(1)
-        before(0)
+        before(1)
         limit(1)
+        negative(1)
+        before(0)
         limit(0)
+        negative(0)
         start(1)
         behind(1)
         start(0)
@@ -271,74 +327,66 @@ def rank_program(g, core, T, topo):
             inv[0] = run("V", vec.tensor_scalar(T.inv16[:, :], T.inv32[:, :], 0.25 - OFF, 0.0, OP.add, OP.max))
         both(0)
         for i in range(2):
-            sc = run("A", act.activation(bank(T.sc, i), bank(T.dwin, same[i]), AF.Sign))
+            sc = run("A", act.activation(bank(T.sc, i), bank(dwin, same[i]), AF.Sign))
         dst = T["Rs%d" % r]
-        need("V", w[0], sc, inv[0])
-        need("A", w[0], inv[0])
-        rs, tail = by_slots(2 * r + 1, T.C2[:, 0:2 * NJ], T.inv16, dst, T["Lr%d" % r], T.sc)
+        got = by_slots(2 * r + 1, T.C2[:, 0:2 * NJ], T.inv16, (dst, T["Lr%d" % r], T["Xr%d" % r], T["Rv%d" % r]), [w[1], w[0], inv[0], sc])
         if r == 0:
             for i in range(2):
-                so = run("A", act.activation(bank(T.so, i), bank(T.dwin, diff[i]), AF.Sign))
+                so = run("A", act.activation(bank(T.so, i), bank(dwin, diff[i]), AF.Sign))
             for i in range(2):
                 sv[0] = run("A", act.activation(bank(T.sv0, i), bank(T.Tg0, diff[i]), AF.Sign, bias=0.5))
             need("A", eyes)
             ni[0] = run("A", act.activation(T.NI[:, :], eye, AF.Copy, scale=-1.0))
-            need("V", rs, so)
+            need("V", so, *got.values())
             for i in range(2):
                 rf[0] = run("V", vec.tensor_tensor(bank(T.Rf, i), bank(dst, diff[i]), bank(T.so, i), OP.mult))
-        return rs
+        return got[0]
 
     def variables(r, rs, out):
-        done = turned(2 * r + 1, AT_VARS, T["Rs%d" % r], rs, T["Lr%d" % r], -1, False)
-        rv, ev = T["Rv%d" % r], {}
-        need("V", sv[0])
-        for d in AT_VARS:
-            if d & 2:
-                need("V", done[d])
-                ev[d] = run("V", vec.tensor_tensor(blk(rv, me ^ d), ps(d), half(T["sv%d" % r], me ^ d), OP.mult))
-            else:
-                need("A", done[d])
-                ev[d] = run("A", act.activation(blk(rv, me ^ d), ps(d), AF.Copy))
+        rv = T["Rv%d" % r]
+        ev = taken(2 * r + 1, T["Rs%d" % r], rs, T["Lr%d" % r], rv)
         gd = T["Gv%d" % r]
         need("V", vl16, *ev.values())
         need("A", vl16, *ev.values())
 
-        def quarter(d):
-            return gd[:, 256 * d:256 * d + 256], rv[:, 0:W].indirect(T.vl16[:, 16 * d:16 * d + 16])
+        def piece(d, lo=0, hi=256):
+            return gd[:, 256 * d + lo:256 * d + hi], rv[:, 0:W].indirect(T.vl16[:, 16 * d + lo // 16:16 * d + hi // 16])
 
-        got = {}
-        for d in range(2):
-            got[d] = run("V", vec.tensor_copy(*quarter(d)))
-            got[d + 2] = run("A", act.activation(*quarter(d + 2), AF.Copy))
+        o, i = piece(0)
+        g0 = run("V", vec.tensor_tensor(o, i, T.xs[:, :], OP.add))
+        g3 = [run("V", vec.tensor_copy(*piece(3, 128, 256)))]
+        g2 = run("A", act.activation(*piece(2), AF.Copy))
+        g3.append(run("A", act.activation(*piece(3, 0, 128), AF.Copy)))
+        need("V", g0)
+        o, i = piece(1)
+        g1 = run("V", vec.tensor_tensor(o, i, gd[:, 0:256], OP.add))
         tt = T.bk0[:, 0:256]
-        need("P", x_in, ev[0])
-        run("P", ten.matmul(tt, eye, T.xs[:, :], True, False))
-        for d in (0, 2, 3):
-            need("P", got[d])
-            t = run("P", ten.matmul(tt, eye, gd[:, 256 * d:256 * d + 256], False, d == 3))
-        need("V", got[1], t)
-        return [run("V", vec.tensor_tensor(out[:, :], tt, gd[:, 256:512], OP.add))]
+        need("P", ev[0], g2)
+        run("P", ten.matmul(tt, eye, gd[:, 512:768], True, False))
+        need("P", *g3)
+        t = run("P", ten.matmul(tt, eye, gd[:, 768:1024], False, True))
+        need("V", g1, t)
+        return run("V", vec.tensor_tensor(out[:, :], tt, gd[:, 256:512], OP.add))
 
-    def own_r(p):
-        return blk(T.Rs0, p) if p // 2 in same else half(T.Rf, p)
-
-    inv, rf, sv, ni = [None], [None], [None], [None]
     rs = check(0, own)
     tw = variables(0, rs, T.Tw)
-    need("P", ni[0], *tw)
+    need("G", tw)
+    send_raw(2, T.Tw)
+    need("P", ni[0], tw)
     sg = [bank(T["bk%d" % (6 + i)], 0) for i in range(2)]
     for i in range(2):
         run("P", ten.matmul(sg[i], T.NI[:, :], bank(T.Rv0, diff[i]), True, False))
-    less_own(range(6))
-    own, tail = var_gather(1, T.Tw, tw)
-    need("P", own, tail)
+    less_own((2, 3, RAW))
+    got = by_slots(2, T.Tw[:, 0:256], T.sn16, (T.Tg1, T.Lm1, T.Xm1, T.Dw1), [tw])
+    need("P", *got.values())
     for i in range(2):
         t = run("P", ten.matmul(sg[i], eye, bank(T.Tg1, diff[i]), False, True))
         need("A", t)
         sv[0] = run("A", act.activation(bank(T.sv1, i), sg[i], AF.Sign, bias=0.5))
-    rs = check(1, own)
+    gather_raw(2)
+    rs = check(1, got[0])
     yt = variables(1, rs, T.ys)
-    need("S", *yt)
+    need("S", yt)
     g.sync.dma_start(T.y[:, :], T.ys[:, :]).then_inc(T.sem.dy, 16)
     need("S", ("dy", 16))
     for q in ("V", "A", "P", "G"):

from concourse.bass import DstId, RemoteDMATransfer
from concourse.mybir import dt, AluOpType, AxisListType, ActivationFunctionType

NR, CAP, V, M = 8, 160, 256, 128
W = NR * CAP
BK = 2 * CAP
H = 2 * BK
NJ = 9 * M
NH = NJ // 2
B = 51.0
OFF = 64
OP = AluOpType
AF = ActivationFunctionType
RAW = 5
TO_CHECKS = {"V": "g7 g4 g1 g0", "A": "g3 g2 g6 c4 c1", "recv": "V0 A5 V7 A3 V2 A6",
             "calls": [[(5, 0, 8)], [(7, 0, 4), (3, 4, 4)], [(6, 0, 4), (2, 4, 4)], [(4, 0, 4), (1, 4, 4)]]}
TO_VARS = {"V": "g7 g5 g4 g1 g0", "A": "g3 g2 g6 c5 c4 c1", "recv": "A0 V3 V7 V2 V6",
           "calls": [[(3, 0, 8)], [(7, 0, 4), (2, 4, 4)], [(6, 0, 4), (5, 4, 4)], [(4, 0, 4), (1, 4, 4)]]}
PLAN = {0: dict(TO_CHECKS, recv="V0 A7 A3 V5 V2 A6"), 1: TO_VARS, 2: TO_CHECKS, 3: TO_VARS}

SCRATCH = {
    "sn32": ("sbuf", [128, 80], "int32"), "pl32": ("sbuf", [128, 64], "int32"), "vl32": ("sbuf", [128, 64], "int32"),
    "sn16": ("sbuf", [128, 80], "uint16"), "pl16": ("sbuf", [128, 64], "uint16"), "vl16": ("sbuf", [128, 64], "uint16"),
    "rn32": ("sbuf", [128, 10], "int32"), "rn16": ("sbuf", [128, 10], "uint16"),
    "ta": ("sbuf", [128, 64], "int32"), "tb": ("sbuf", [128, 64], "int32"), "tc": ("sbuf", [128, 64], "int32"),
    "td": ("sbuf", [128, 64], "int32"), "pc16": ("sbuf", [128, 64], "uint16"),
    "num": ("sbuf", [128, 512], "float32"), "num2": ("sbuf", [128, 512], "float32"),
    "iva": ("sbuf", [128, W], "float32"), "ivb": ("sbuf", [128, W], "float32"),
    "inv32": ("sbuf", [128, 80], "float32"), "inv16": ("sbuf", [128, 80], "uint16"),
    "one": ("sbuf", [128, 256], "bfloat16"), "E": ("sbuf", [128, 256], "bfloat16"), "NI": ("sbuf", [128, 128], "bfloat16"),
    "xs": ("sbuf", [128, 256], "bfloat16"), "Tw": ("sbuf", [128, 256], "bfloat16"), "ys": ("sbuf", [128, 256], "float32"),
    "D": ("sbuf", [128, NJ], "bfloat16"), "A": ("sbuf", [128, NJ], "bfloat16"), "NA": ("sbuf", [128, NJ], "bfloat16"),
    "F": ("sbuf", [128, NJ], "bfloat16"), "Z": ("sbuf", [128, NH], "bfloat16"),
    "C0": ("sbuf", [128, 2 * NJ], "bfloat16"), "C1": ("sbuf", [128, 2 * NJ], "bfloat16"), "C2": ("sbuf", [128, 2 * NJ], "bfloat16"),
    "sc": ("sbuf", [128, H], "bfloat16"), "so": ("sbuf", [128, H], "bfloat16"), "Rf": ("sbuf", [128, H], "bfloat16"),
}
for _d in range(NR):
    SCRATCH["bk%d" % _d] = ("psum", [128, 512], "float32")
for _r in range(2):
    for _n, _w in (("Tg", W), ("Rs", W), ("Lm", W), ("Lr", W), ("Xm", W), ("Xr", W), ("Dw", W), ("Rv", W), ("Gv", 1024), ("sv", H),
                   ("rx", 256)):
        SCRATCH["%s%d" % (_n, _r)] = ("sbuf", [128, _w], "bfloat16")
SEMAPHORES = ["sV", "sA", "sP", "sG", "dx", "dsn", "dpl", "dvl", "df", "dr", "da", "dy", "ls", "rn"]
SEMAPHORES += ["arr%d_%d" % (ph, p) for ph in range(4) for p in range(NR)]


def rank_program(g, core, T, topo):
    me = T.rank_of(core)
    if me is None:
        return
    queue = {"V": g.vector, "A": g.scalar, "P": g.tensor, "G": g, "S": g.sync}
    cnt = {"V": 0, "A": 0, "P": 0, "G": 0, "ls": 0}
    seen = {}
    vec, act, ten = g.vector, g.scalar, g.tensor

    def need(q, *toks):
        for sem, val in toks:
            if seen.get((q, sem), 0) < val:
                queue[q].wait_ge(T.sem[sem], val)
                seen[(q, sem)] = val

    def run(q, inst):
        cnt[q] += 1
        inst.then_inc(T.sem["s" + q], 1)
        return ("s" + q, cnt[q])

    s0 = me // 2
    same = [s0, s0 ^ 2]
    diff = [s0 ^ 1, s0 ^ 3]

    def bank(buf, b):
        return buf[:, b * BK:(b + 1) * BK]

    def blk(buf, q):
        return buf[:, q * CAP:(q + 1) * CAP]

    def half(buf, q):
        b = q // 2
        return blk(buf, 2 * (same.index(b) if b in same else diff.index(b)) + q % 2)

    def ps(d):
        return T["bk%d" % d][:, 0:CAP]

    def turn(ph, r):
        k = me * r if ph % 2 == 0 else -me * r
        s = (128 - 16 * (k % 8)) % 128
        return T.E[:, s:s + 128]

    def const(ap, n, value):
        return run("G", g.iota(ap, [[0, n]], value, 0, allow_small_or_imprecise_dtypes=True))

    eye = T.E[:, 0:128]
    g.sync.dma_start(T.sn32[:, :], T.sn[:, :]).then_inc(T.sem.dsn, 16)
    act.dma_start(T.xs[:, :], T.x[:, :]).then_inc(T.sem.dx, 16)
    g.sync.dma_start(T.pl32[:, :], T.pl[:, :]).then_inc(T.sem.dpl, 16)
    act.dma_start(T.vl32[:, :], T.vl[:, :]).then_inc(T.sem.dvl, 16)
    sn_in, x_in, pl_in, vl_in = ("dsn", 16), ("dx", 16), ("dpl", 16), ("dvl", 16)
    num = run("G", g.iota(T.num[:, :], [[2, 4], [18, 128]], 1 + OFF, 0, allow_small_or_imprecise_dtypes=True))
    ones = run("V", vec.memset(T.one[:, :], 1.0))
    need("G", ones)
    eyes = run("G", g.affine_select(T.E[:, :], T.one[:, :], [[0, 2], [-1, 128]], OP.is_equal, 0.0, 0, 1))
    need("A", ones)
    run("A", act.activation(T.C1[:, 1:2 * NJ:NJ], T.one[:, 0:2], AF.Silu, bias=B - 1.0))
    zero = run("V", vec.memset(T.Z[:, :], 0.0))
    fill = run("V", vec.memset(T.iva[:, :], 0.0))
    need("S", fill)
    g.sync.dma_start(T.ivb[0:128:16, :], T.iva[0:128:16, :]).then_inc(T.sem.df, 16)
    need("V", sn_in)
    sn16 = run("V", vec.tensor_copy(T.sn16[:, :], T.sn32[:, :]))

    def toks(ph, name, kind=None):
        return [(t[0], int(t[1:])) for t in PLAN[ph][name].split() if kind is None or t[0] == kind]

    def turned_here(ph):
        return [d for q in "VA" for k, d in toks(ph, q, "c")]

    def arrived(ph, d):
        return ("arr%d_%d" % (ph, me ^ d), [n for c in PLAN[ph]["calls"] for e, o, n in c if e == d][0])

    def send(items):
        tr = []
        for d, o, n, src, dst, sem in items:
            to = T.cores[me ^ d]
            rid, pid, _s = topo.addr(to)
            tr.append(RemoteDMATransfer(dst_ids=[DstId(rid=rid, pnc=pid)], dma_engine_mask=sum(1 << e for e in topo.engines(core, to)[o:o + n]),
                                        remote_sem=T.sem[sem], src=src, dst=dst))
            cnt["ls"] += n
        g.remote_dma_fused(tr, local_sem=T.sem.ls)

    def send_raw(ph, win):
        d, o, n = PLAN[ph]["calls"][0][0]
        send([(d, o, n, win[:, :], T["rx%d" % (ph // 2)][:, :], "arr%d_%d" % (ph, me))])

    def drain(ph, q, out, src):
        if ph % 2 == 0:
            if q == "V":
                return run("V", vec.tensor_scalar(out, src, 2.0, 1.0, OP.mult, OP.add))
            return run("A", act.activation(out, src, AF.Identity, bias=1.0, scale=2.0))
        if q == "V":
            return run("V", vec.tensor_copy(out, src))
        return run("A", act.activation(out, src, AF.Copy))

    def by_slots(ph, win, lst, bufs, ready):
        src, land, xsrc, xland = bufs
        xs, got, out, trn = turned_here(ph), {}, {}, {}
        need("V", *ready)
        need("A", *ready)

        def gather(q, d):
            r = me ^ d
            i, o = win.indirect(lst[:, r * CAP // 16:(r + 1) * CAP // 16]), blk(src, r)
            if q == "A":
                return run("A", act.activation(o, i, AF.Copy))
            if ph == 2 and not d & 2:
                return run("V", vec.tensor_tensor(o, i, blk(T.Rv0, r), OP.subtract))
            if ph % 2 and not d & 2:
                return run("V", vec.tensor_tensor(o, i, half(T.sc, r), OP.mult))
            return run("V", vec.tensor_copy(o, i))

        todo = {q: toks(ph, q) for q in "VA"}
        while todo["V"] or todo["A"]:
            for q in "VA":
                while todo[q] and (todo[q][0][0] == "g" or todo[q][0][1] in trn):
                    kind, d = todo[q].pop(0)
                    r = me ^ d
                    if kind == "c":
                        need(q, trn[d])
                        out[d] = drain(ph, q, blk(xsrc, r), ps(d))
                        continue
                    got[d] = gather(q, d)
                    if d in xs:
                        need("P", eyes, got[d])
                        trn[d] = run("P", ten.matmul(ps(d), turn(ph, r), blk(src, r), True, True))
        for c in PLAN[ph]["calls"][(ph + 1) % 2:]:
            for d, o, n in c:
                need("G", out[d] if d in xs else got[d])
            send([(d, o, n, blk(xsrc if d in xs else src, me ^ d), blk(xland if d in xs else land, me), "arr%d_%d" % (ph, me))
                  for d, o, n in c])
        return got

    def taken(ph, mine, mine_ready, land, rv, early=None):
        done, ev, left = {}, {}, [early] if early else []
        for q, d in toks(ph, "recv"):
            p = me ^ d
            need("P", rawg[ph] if (ph, d) in ((0, RAW), (2, RAW)) else arrived(ph, d) if d else mine_ready)
            done[d] = run("P", ten.matmul(ps(d), turn(ph, p), blk(land if d else mine, p), not (ph == 2 and (d & 2 or d == RAW)), True))
            if left:
                left.pop()()
        for q, d in toks(ph, "recv"):
            p = me ^ d
            need(q, done[d])
            if ph % 2 and d & 2:
                need("V", sv[0])
                ev[d] = run("V", vec.tensor_tensor(blk(rv, p), ps(d), half(T["sv%d" % (ph // 2)], p), OP.mult))
            else:
                ev[d] = drain(ph, q, blk(rv, p), ps(d))
        for d in turned_here(ph):
            ev[d] = arrived(ph, d)
        return ev

    def gather_raw(ph):
        need("V", arrived(ph, RAW))
        win = T["rx%d" % (ph // 2)][:, 0:256]
        rawg[ph] = run("V", vec.tensor_copy(blk(T["Lm%d" % (ph // 2)], me ^ RAW), win.indirect(T.rn16[:, :])))

    inv, rf, sv, ni, rawg = [None], [None], [None], [None], {}
    need("G", x_in)
    send_raw(0, T.xs)
    need("G", sn_in)
    send([(RAW, 0, 8, T.sn32[:, (me ^ RAW) * 10:(me ^ RAW) * 10 + 10], T.rn32[:, :], "rn")])
    own = by_slots(0, T.xs[:, 0:256], T.sn16, (T.Tg0, T.Lm0, T.Xm0, T.Dw0), [sn16, x_in])[0]
    need("A", num)
    num2 = run("A", act.activation(T.num2[:, :], T.num[:, :], AF.Silu, bias=8.0))
    need("V", pl_in)
    ta = run("V", vec.tensor_scalar(T.ta[:, :], T.pl32[:, :], 15, None, OP.bitwise_and))
    tb = run("V", vec.tensor_scalar(T.tb[:, :], T.pl32[:, :], 4, None, OP.arith_shift_right))
    need("V", ta)
    tc = run("V", vec.tensor_scalar(T.tc[:, :], T.ta[:, :], 80.0, None, OP.mult))
    pl16 = run("V", vec.tensor_copy(T.pl16[:, :], T.pl32[:, :]))
    need("V", tb, tc)
    td = run("V", vec.tensor_tensor(T.td[:, :], T.tc[:, :], T.tb[:, :], OP.add))
    need("V", vl_in)
    vl16 = run("V", vec.tensor_copy(T.vl16[:, :], T.vl32[:, :]))
    need("V", td)
    pc = run("V", vec.tensor_copy(T.pc16[:, :], T.td[:, :]))
    need("V", pc, fill, num, ("df", 16))
    scat = run("V", vec.tensor_copy(T.iva[:, 0:W].indirect(T.pc16[:, 0:32]), T.num[:, :]))
    need("A", pc, num2, ("df", 16))
    scat2 = run("A", act.activation(T.ivb[:, 0:W].indirect(T.pc16[:, 32:64]), T.num2[:, :], AF.Silu))
    need("S", scat)
    g.sync.dma_start(T.inv32[:, :], T.iva[0:128:16, :]).then_inc(T.sem.dr, 16)
    need("V", ("rn", 8))
    rn16 = run("V", vec.tensor_copy(T.rn16[:, :], T.rn32[:, :]))
    need("V", rn16)
    gather_raw(0)
    need("G", zero)
    const(T.Z[:, 8:NH:9], M // 2, int(B))
    const(T.D[:, 8:NJ:9], M, 0)
    z = const(T.C1[:, NJ - 2:2 * NJ:NJ], 2, 0)
    c0 = {k: const(T.C0[:, k * NJ:(k + 1) * NJ:2], NH, 64) for k in (1, 0)}
    need("G", scat2, ("dr", 16))
    g.dma_start(T.inv32[:, :], T.ivb[0:128:16, :], accum_op=OP.add).then_inc(T.sem.da, 16)

    def less_own(ds):
        need("P", ni[0], rf[0])
        for d in ds:
            run("P", ten.matmul(ps(d), T.NI[:, :], half(T.Rf, me ^ d) if d & 2 else blk(T.Rs0, me ^ d), True, False))

    def check(r, mine_ready):
        dwin = T["Dw%d" % r]

        def late():
            need("P", sv[0])
            less_own((6, 7))

        ev = taken(2 * r, T["Tg%d" % r], mine_ready, T["Lm%d" % r], dwin, late if r else None)
        win = dwin[:, 0:W]
        need("V", pl16, *ev.values())
        need("A", pl16, *ev.values())
        for e in range(4):
            gv = run("V", vec.tensor_copy(T.D[:, e:NJ:9], win.indirect(T.pl16[:, 8 * e:8 * e + 8])))
            ga = run("A", act.activation(T.D[:, e + 4:NJ:9], win.indirect(T.pl16[:, 8 * e + 32:8 * e + 40]), AF.Copy))
        need("V", gv, ga, z)
        need("A", gv, ga, z)

        def part(buf, k):
            return buf[:, k * NH:(k + 1) * NH]

        ab, na, lim, neg, suf, w, fs, f, pre = {}, {}, {}, {}, {}, {}, {}, {}, {}
        for k in (1, 0):
            f[k] = run("V", vec.tensor_tensor_scan(part(T.F, k), part(T.D, k), T.Z[:, :], B, OP.mult, OP.add))
            ab[k] = run("A", act.activation(part(T.A, k), part(T.D, k), AF.Abs, bias=-0.5, scale=0.5))

        def before(k):
            need("V", ab[k])
            lo, hi = k * NH + 1, (k + 1) * NH
            pre[k] = run("V", vec.tensor_tensor_scan(T.C1[:, 2 * lo + 1:2 * hi:2], T.A[:, lo - 1:hi - 1], T.Z[:, :NH - 1], B, OP.min, OP.max))

        def negative(k):
            lo, hi = k * NH + 1, (k + 1) * NH
            need("A", pre[k], c0[k])
            neg[k] = run("A", act.activation(T.C0[:, 2 * lo - 1:2 * hi:2], T.C1[:, 2 * lo - 1:2 * hi:2], AF.Copy, scale=-1.0))

        def negate(k):
            if k:
                need("V", ab[k])
                na[k] = run("V", vec.tensor_scalar(part(T.NA, k), part(T.A, k), -1.0, None, OP.mult))
            else:
                need("A", ab[k])
                na[k] = run("A", act.activation(part(T.NA, k), part(T.A, k), AF.Copy, scale=-1.0))

        def limit(k):
            need("G", na[k])
            lim[k] = const(T.NA[:, k * NH + 8:(k + 1) * NH:9], M // 2, 64)

        def start(k):
            lo, hi = k * NH, (k + 1) * NH
            need("V", f[k], na[k], pre[k])
            fs[k] = run("V", vec.tensor_copy(T.A[:, lo + 8:hi:9], T.F[:, lo + 7:hi:9]))

        def behind(k):
            need("V", fs[k], lim[k])
            top = (k + 1) * NH - 1
            cols, to = slice(top, k * NH, -1), slice(2 * (top - 1), 2 * k * NH - 2 if k else None, -2)
            suf[k] = run("V", vec.tensor_tensor_scan(T.C1[:, to], T.NA[:, cols], T.A[:, cols], 0.0, OP.max, OP.min))

        def both(k):
            need("V", suf[k], neg[k])
            c = slice(2 * k * NH, 2 * (k + 1) * NH)
            w[k] = run("V", vec.tensor_tensor_scan(T.C2[:, c], T.C0[:, c], T.C1[:, c], 0.0, OP.max, OP.min))

        negate(0)
        negate(1)
        before(1)
        limit(1)
        negative(1)
        before(0)
        limit(0)
        negative(0)
        start(1)
        behind(1)
        start(0)
        behind(0)
        both(1)
        if r == 0:
            need("V", ("da", 16))
            inv[0] = run("V", vec.tensor_scalar(T.inv16[:, :], T.inv32[:, :], 0.25 - OFF, 0.0, OP.add, OP.max))
        both(0)
        for i in range(2):
            sc = run("A", act.activation(bank(T.sc, i), bank(dwin, same[i]), AF.Sign))
        dst = T["Rs%d" % r]
        got = by_slots(2 * r + 1, T.C2[:, 0:2 * NJ], T.inv16, (dst, T["Lr%d" % r], T["Xr%d" % r], T["Rv%d" % r]), [w[1], w[0], inv[0], sc])
        if r == 0:
            for i in range(2):
                so = run("A", act.activation(bank(T.so, i), bank(dwin, diff[i]), AF.Sign))
            for i in range(2):
                sv[0] = run("A", act.activation(bank(T.sv0, i), bank(T.Tg0, diff[i]), AF.Sign, bias=0.5))
            need("A", eyes)
            ni[0] = run("A", act.activation(T.NI[:, :], eye, AF.Copy, scale=-1.0))
            need("V", so, *got.values())
            for i in range(2):
                rf[0] = run("V", vec.tensor_tensor(bank(T.Rf, i), bank(dst, diff[i]), bank(T.so, i), OP.mult))
        return got[0]

    def variables(r, rs, out):
        rv = T["Rv%d" % r]
        ev = taken(2 * r + 1, T["Rs%d" % r], rs, T["Lr%d" % r], rv)
        gd = T["Gv%d" % r]
        need("V", vl16, *ev.values())
        need("A", vl16, *ev.values())

        def piece(d, lo=0, hi=256):
            return gd[:, 256 * d + lo:256 * d + hi], rv[:, 0:W].indirect(T.vl16[:, 16 * d + lo // 16:16 * d + hi // 16])

        o, i = piece(0)
        g0 = run("V", vec.tensor_tensor(o, i, T.xs[:, :], OP.add))
        g3 = [run("V", vec.tensor_copy(*piece(3, 128, 256)))]
        g2 = run("A", act.activation(*piece(2), AF.Copy))
        g3.append(run("A", act.activation(*piece(3, 0, 128), AF.Copy)))
        need("V", g0)
        o, i = piece(1)
        g1 = run("V", vec.tensor_tensor(o, i, gd[:, 0:256], OP.add))
        tt = T.bk0[:, 0:256]
        need("P", ev[0], g2)
        run("P", ten.matmul(tt, eye, gd[:, 512:768], True, False))
        need("P", *g3)
        t = run("P", ten.matmul(tt, eye, gd[:, 768:1024], False, True))
        need("V", g1, t)
        return run("V", vec.tensor_tensor(out[:, :], tt, gd[:, 256:512], OP.add))

    rs = check(0, own)
    tw = variables(0, rs, T.Tw)
    need("G", tw)
    send_raw(2, T.Tw)
    need("P", ni[0], tw)
    sg = [bank(T["bk%d" % (6 + i)], 0) for i in range(2)]
    for i in range(2):
        run("P", ten.matmul(sg[i], T.NI[:, :], bank(T.Rv0, diff[i]), True, False))
    less_own((2, 3, RAW))
    got = by_slots(2, T.Tw[:, 0:256], T.sn16, (T.Tg1, T.Lm1, T.Xm1, T.Dw1), [tw])
    need("P", *got.values())
    for i in range(2):
        t = run("P", ten.matmul(sg[i], eye, bank(T.Tg1, diff[i]), False, True))
        need("A", t)
        sv[0] = run("A", act.activation(bank(T.sv1, i), sg[i], AF.Sign, bias=0.5))
    gather_raw(2)
    rs = check(1, got[0])
    yt = variables(1, rs, T.ys)
    need("S", yt)
    g.sync.dma_start(T.y[:, :], T.ys[:, :]).then_inc(T.sem.dy, 16)
    need("S", ("dy", 16))
    for q in ("V", "A", "P", "G"):
        need("G", ("s" + q, cnt[q]))
    need("G", ("ls", cnt["ls"]))
